import numpy as np
import ml_dtypes


def mxq(x, axis, fmt="e4m3"):
    dtype, down = {"e4m3": (ml_dtypes.float8_e4m3fn, 7), "e5m2": (ml_dtypes.float8_e5m2, 14)}[fmt]
    v = np.moveaxis(np.asarray(x, np.float32).astype(ml_dtypes.bfloat16).astype(np.float64), axis, -1)
    blocks = v.reshape(v.shape[:-1] + (-1, 32))
    amax = np.abs(blocks).max(-1, keepdims=True)
    byte = np.maximum(np.where(amax > 0, np.frexp(amax)[1] - 1 + 127, 0) - down, 1)
    scale = np.exp2(byte - 127.0)
    codes = (blocks / scale).astype(np.float32).astype(dtype).astype(np.float64)
    return np.moveaxis((codes * scale).reshape(v.shape), -1, axis)


WIDE = False


def mx_kscale(k):
    if not WIDE:
        return np.ones(k)
    levels = np.array([10, -10, 5, -5, 0])
    if k % 512:
        return np.exp2(np.random.permutation(np.resize(levels, k // 32))).repeat(32)
    a = np.empty((k // 512, 16))
    for p in range(k // 512):
        a[p, :8] = np.random.permutation(np.resize(levels, 8))
        for g in range(8):
            far = levels[np.abs(levels - a[p, g]) >= 10]
            a[p, g + 8] = far[np.random.randint(len(far))]
    return np.exp2(a.ravel()).repeat(32)


def f64(x):
    return np.asarray(x).astype(np.float64)


def striped(idx):
    return np.tile(idx.reshape(-1, 16).T, (8, 1)).astype(np.uint16)


def unstriped(offs):
    return offs[:16].T.reshape(-1).astype(np.int64)


E2M1 = np.array([0.0, 0.5, 1.0, 1.5, 2.0, 3.0, 4.0, 6.0, -0.0, -0.5, -1.0, -1.5, -2.0, -3.0, -4.0, -6.0])


def pack_weight(w, fmt):
    k, n = w.shape
    w = f64(np.asarray(w, np.float32).astype(ml_dtypes.bfloat16)).reshape(k // 32, 32, n)
    amax = np.abs(w).max(1)
    if fmt == "e4m3":
        byte = np.frexp(amax)[1] - 1 + 127 - 7
    else:
        mant, ex = np.frexp(amax / 6.0)
        byte = np.where(mant > 0.5, ex, ex - 1) + 127
    byte = np.clip(np.where(amax > 0, byte, 1), 1, 254)
    scaled = (w * np.exp2(127.0 - byte)[:, None, :]).reshape(k, n).astype(np.float32)
    by_word = np.ascontiguousarray(scaled.reshape(k // 512, 128, 4, n).transpose(0, 1, 3, 2))
    if fmt == "e4m3":
        words = by_word.astype(ml_dtypes.float8_e4m3fn).view(np.uint8)
    else:
        c = by_word.astype(ml_dtypes.float4_e2m1fn).view(np.uint8) & 0xF
        words = (c[..., 0::2] | (c[..., 1::2] << 4)).reshape(k // 512, 128, 2 * n)
    return np.ascontiguousarray(words), np.ascontiguousarray(byte.astype(np.uint8).reshape(k // 512, 16, n))


def unpack_weight(words, scales, fmt):
    g, _, n = scales.shape
    words = np.ascontiguousarray(words).reshape(g, 128, n, -1)
    if fmt == "e4m3":
        vals = words.view(ml_dtypes.float8_e4m3fn).astype(np.float64)
    else:
        nib = np.empty((g, 128, n, 4), np.uint8)
        nib[..., 0::2] = words & 0xF
        nib[..., 1::2] = words >> 4
        vals = E2M1[nib]
    vals = vals * np.repeat(np.exp2(scales.astype(np.float64) - 127.0), 8, axis=1)[..., None]
    return vals.transpose(0, 1, 3, 2).reshape(g * 512, n)


def gelu(v):
    return 0.5 * v * (1.0 + np.tanh(np.sqrt(2.0 / np.pi) * (v + 0.044715 * v**3)))


K, T, E, C, N = 2048, 512, 6, 128, 512


def by_slot(wq, xq):
    return np.concatenate([xq[:, e * C:(e + 1) * C].T @ wq[e] for e in range(E)])


def setup_inputs():
    n = np.random.standard_normal
    s = mx_kscale(K)
    slot_token = np.concatenate([np.random.permutation(T)[:C] for e in range(E)])
    x = pack_weight(n((K, T)) * s[:, None], "e2m1")
    two = np.ascontiguousarray(x[0].reshape(K // 1024, 2, 128, T, 2).transpose(0, 2, 3, 1, 4).reshape(K // 1024, 128, T, 4))
    return {
        "x_words": two,
        "x_scales": x[1],
        "w": (n((E, K, N)) / np.sqrt(K) / s[None, :, None]).astype(np.float32),
        "w3": (n((E, K, N)) / np.sqrt(K) / s[None, :, None]).astype(np.float32),
        "offs": striped(slot_token),
    }


def reference(x_words, x_scales, w, w3, offs):
    wq = mxq(f64(w), 1, "e4m3")
    w3q = mxq(f64(w3), 1, "e4m3")
    idx = unstriped(offs)
    words = x_words.reshape(K // 1024, 128, T, 2, 2).transpose(0, 3, 1, 2, 4).reshape(K // 512, 128, 2 * T)
    xq = unpack_weight(words, x_scales, "e2m1")[:, idx]
    y = gelu(by_slot(wq, xq)) * by_slot(w3q, xq)
    return y

@@ -1,0 +1,138 @@
+from contextlib import ExitStack
+
+import concourse.mybir as mybir
+
+K, T, E, C, N = 2048, 512, 6, 128, 512
+SLOTS = E * C
+
+F32 = mybir.dt.float32
+BF16 = mybir.dt.bfloat16
+I32 = mybir.dt.int32
+U32 = mybir.dt.uint32
+U16 = mybir.dt.uint16
+U8 = mybir.dt.uint8
+FP8X4 = mybir.dt.float8_e4m3fn_x4
+FP4X4 = mybir.dt.float4_e2m1fn_x4
+GELU = mybir.ActivationFunctionType.Gelu_apprx_tanh
+MULT = mybir.AluOpType.mult
+
+P = 128
+PACK = 4
+K_PASS = P * PACK
+PASSES = K // K_PASS
+PAIRS = PASSES // 2
+GATHER = 384
+VECTOR_COLUMNS = 256
+RUN = 4
+
+FLOPS = 2 * 2 * SLOTS * K * N
+
+
+def passes_per_load(expert, matrix):
+    if expert < E - 1:
+        return [4]
+    return [2, 2] if matrix == 0 else [1, 1, 1, 1]
+
+
+def tile_moe_s_glu_gelu_kernel(tc, x_words, x_scales, w, w3, offs, out):
+    nc = tc.nc
+
+    with ExitStack() as ctx:
+        keep = ctx.enter_context(tc.tile_pool(name="keep", bufs=1))
+        raw_pool = ctx.enter_context(tc.tile_pool(name="raw", bufs=4))
+        stage = ctx.enter_context(tc.tile_pool(name="stage", bufs=4))
+        quant = ctx.enter_context(tc.tile_pool(name="quant", bufs=6))
+        act = ctx.enter_context(tc.tile_pool(name="act", bufs=2))
+        psum = ctx.enter_context(tc.psum_pool(name="psum", bufs=2))
+
+        offsets = keep.tile([P, SLOTS // 16], U16, name="offsets")
+        token_words = keep.tile([P, PAIRS, T], I32, name="token_words", align_bytes=64)
+        token_scales = keep.tile([P, PASSES, T], U8, name="token_scales", align_bytes=64)
+        slot_pairs = keep.tile([P, PAIRS, SLOTS], U32, name="slot_pairs", align_bytes=64)
+        slot_words = keep.tile([P, PASSES, 2 * SLOTS], U8, name="slot_words", align_bytes=64)
+        slot_scales = keep.tile([P, PASSES, SLOTS], U8, name="slot_scales", align_bytes=64)
+        early_out = keep.tile([P, E - 1, N], F32, name="early_out")
+        last_out = keep.tile([P, N], F32, name="last_out")
+
+        nc.sync.dma_start(
+            out=token_words[:],
+            in_=x_words.rearrange("m p t d -> p m (t d)").bitcast(I32),
+        )
+        nc.sync.dma_start(offsets[:], offs)
+
+        nc.vector.memset(token_scales[:].rearrange("p s t -> p (s t)").bitcast(I32), 0)
+        for q in range(4):
+            nc.scalar.dma_start(
+                out=token_scales[32 * q : 32 * q + 4, :, :].bitcast(I32),
+                in_=x_scales[:, 4 * q : 4 * q + 4, :].rearrange("s b t -> b s t").bitcast(I32),
+            )
+
+        for j0 in range(0, SLOTS, GATHER):
+            piece = offsets[:, j0 // 16 : (j0 + GATHER) // 16]
+            for m in range(PAIRS):
+                nc.vector.tensor_copy(
+                    slot_pairs[:, m, j0 : j0 + GATHER],
+                    token_words[:, m, :].bitcast(U32).indirect(piece),
+                )
+            for s in range(PASSES):
+                nc.vector.tensor_copy(
+                    slot_scales[:, s, j0 : j0 + GATHER],
+                    token_scales[:, s, :].indirect(piece),
+                )
+        for m in range(PAIRS):
+            nc.vector.tensor_copy(
+                slot_words[:, 2 * m : 2 * m + 2, :].bitcast(U16),
+                slot_pairs[:, m, :].bitcast(U16).rearrange("p (j q) -> p q j", q=2),
+            )
+
+        for e in range(E):
+            for matrix, weights in enumerate((w, w3)):
+                raw = raw_pool.tile([P, PASSES, PACK, N], F32, name="raw")
+                s0 = 0
+                for count in passes_per_load(e, matrix):
+                    rows = weights[e, K_PASS * s0 : K_PASS * (s0 + count), :]
+                    nc.sync.dma_start(
+                        out=raw[:, s0 : s0 + count].rearrange("p s r n -> p s (r n)"),
+                        in_=rows.rearrange("(s p r) n -> p s (r n)", p=P, r=PACK),
+                    )
+                    s0 += count
+
+                acc = psum.tile([P, N], F32, name="acc%d" % matrix)
+                for s in range(PASSES):
+                    grouped = stage.tile([P, N, PACK], BF16, name="grouped", align_bytes=64)
+                    nc.vector.tensor_copy(
+                        out=grouped[:, :VECTOR_COLUMNS, :].rearrange("p (c i) r -> p c r i", i=RUN),
+                        in_=raw[:, s, :, :VECTOR_COLUMNS].rearrange("p r (c i) -> p c r i", i=RUN),
+                    )
+                    nc.scalar.copy(
+                        out=grouped[:, VECTOR_COLUMNS:, :].rearrange("p (c i) r -> p c r i", i=RUN),
+                        in_=raw[:, s, :, VECTOR_COLUMNS:].rearrange("p r (c i) -> p c r i", i=RUN),
+                    )
+                    codes = quant.tile([P, N], U32, name="codes", align_bytes=64)
+                    scales = quant.tile([P, N], U8, name="scales", align_bytes=64)
+                    nc.vector.quantize_mx(
+                        out=codes[:].bitcast(FP8X4),
+                        scales=scales[:],
+                        in_=grouped[:].rearrange("p n r -> p (n r)"),
+                    )
+                    nc.tensor.matmul_mx(
+                        out=acc[:],
+                        lhsT=slot_words[:, s, 2 * C * e : 2 * C * (e + 1)].bitcast(FP4X4),
+                        lhsT_scale=slot_scales[:, s, C * e : C * (e + 1)],
+                        rhs=codes[:].bitcast(FP8X4),
+                        rhs_scale=scales[:],
+                        start=(s == 0),
+                        stop=(s == PASSES - 1),
+                    )
+                if matrix == 0:
+                    gate = act.tile([P, N], F32, name="gate")
+                    nc.scalar.activation(gate[:], acc[:], GELU)
+                else:
+                    result = early_out[:, e, :] if e < E - 1 else last_out[:]
+                    nc.vector.tensor_tensor(result, acc[:], gate[:], MULT)
+
+        nc.sync.dma_start(
+            out=out[: (E - 1) * C, :].rearrange("(e p) n -> p e n", p=P),
+            in_=early_out[:],
+        )
+        nc.sync.dma_start(out=out[(E - 1) * C :, :], in_=last_out[:])

@@ -24,14 +24,16 @@ PAIRS = PASSES // 2
 GATHER = 384
 VECTOR_COLUMNS = 256
 RUN = 4
+QUARTER = N // 4
 
 FLOPS = 2 * 2 * SLOTS * K * N
 
 
-def passes_per_load(expert, matrix):
-    if expert < E - 1:
-        return [4]
-    return [2, 2] if matrix == 0 else [1, 1, 1, 1]
+def interleave(copy, grouped, raw, columns):
+    copy(
+        out=grouped[:, columns, :].rearrange("p (c i) r -> p c r i", i=RUN),
+        in_=raw[:, :, columns].rearrange("p r (c i) -> p c r i", i=RUN),
+    )
 
 
 def tile_moe_s_glu_gelu_kernel(tc, x_words, x_scales, w, w3, offs, out):
@@ -39,11 +41,12 @@ def tile_moe_s_glu_gelu_kernel(tc, x_words, x_scales, w, w3, offs, out):
 
     with ExitStack() as ctx:
         keep = ctx.enter_context(tc.tile_pool(name="keep", bufs=1))
-        raw_pool = ctx.enter_context(tc.tile_pool(name="raw", bufs=4))
+        raw_pool = ctx.enter_context(tc.tile_pool(name="raw", bufs=8))
         stage = ctx.enter_context(tc.tile_pool(name="stage", bufs=4))
         quant = ctx.enter_context(tc.tile_pool(name="quant", bufs=6))
         act = ctx.enter_context(tc.tile_pool(name="act", bufs=2))
         psum = ctx.enter_context(tc.psum_pool(name="psum", bufs=2))
+        last_psum = ctx.enter_context(tc.psum_pool(name="last_psum", bufs=1))
 
         offsets = keep.tile([P, SLOTS // 16], U16, name="offsets")
         token_words = keep.tile([P, PAIRS, T], I32, name="token_words", align_bytes=64)
@@ -85,54 +88,88 @@ def tile_moe_s_glu_gelu_kernel(tc, x_words, x_scales, w, w3, offs, out):
                 slot_pairs[:, m, :].bitcast(U16).rearrange("p (j q) -> p q j", q=2),
             )
 
+        def load(weights, e, queues):
+            count = PASSES // len(queues)
+            halves = [raw_pool.tile([P, 2, PACK, N], F32, name="raw") for half in range(2)]
+            for d, queue in enumerate(queues):
+                s0 = count * d
+                rows = weights[e, K_PASS * s0 : K_PASS * (s0 + count), :]
+                queue.dma_start(
+                    out=halves[s0 // 2][:, s0 % 2 : s0 % 2 + count].rearrange("p s r n -> p s (r n)"),
+                    in_=rows.rearrange("(s p r) n -> p s (r n)", p=P, r=PACK),
+                )
+            return [halves[s // 2][:, s % 2] for s in range(PASSES)]
+
+        def quantize(grouped, columns, codes, scales):
+            nc.vector.quantize_mx(
+                out=codes[:, columns].bitcast(FP8X4),
+                scales=scales[:, columns],
+                in_=grouped[:, columns, :].rearrange("p n r -> p (n r)"),
+            )
+
+        def multiply(acc, e, s, codes, scales, columns):
+            nc.tensor.matmul_mx(
+                out=acc,
+                lhsT=slot_words[:, s, 2 * C * e : 2 * C * (e + 1)].bitcast(FP4X4),
+                lhsT_scale=slot_scales[:, s, C * e : C * (e + 1)],
+                rhs=codes[:, columns].bitcast(FP8X4),
+                rhs_scale=scales[:, columns],
+                start=(s == 0),
+                stop=(s == PASSES - 1),
+            )
+
+        def pass_tiles():
+            grouped = stage.tile([P, N, PACK], BF16, name="grouped", align_bytes=64)
+            codes = quant.tile([P, N], U32, name="codes", align_bytes=64)
+            scales = quant.tile([P, N], U8, name="scales", align_bytes=64)
+            return grouped, codes, scales
+
+        def quantize_pass(raw):
+            grouped, codes, scales = pass_tiles()
+            interleave(nc.vector.tensor_copy, grouped, raw, slice(0, VECTOR_COLUMNS))
+            interleave(nc.scalar.copy, grouped, raw, slice(VECTOR_COLUMNS, N))
+            quantize(grouped, slice(0, N), codes, scales)
+            return codes, scales
+
+        def product(weights, e, queues, name):
+            raws = load(weights, e, queues)
+            acc = psum.tile([P, N], F32, name=name)
+            for s in range(PASSES):
+                codes, scales = quantize_pass(raws[s])
+                multiply(acc[:], e, s, codes, scales, slice(0, N))
+            return acc
+
         for e in range(E):
-            for matrix, weights in enumerate((w, w3)):
-                raw = raw_pool.tile([P, PASSES, PACK, N], F32, name="raw")
-                s0 = 0
-                for count in passes_per_load(e, matrix):
-                    rows = weights[e, K_PASS * s0 : K_PASS * (s0 + count), :]
-                    nc.sync.dma_start(
-                        out=raw[:, s0 : s0 + count].rearrange("p s r n -> p s (r n)"),
-                        in_=rows.rearrange("(s p r) n -> p s (r n)", p=P, r=PACK),
-                    )
-                    s0 += count
+            queues = [nc.sync, nc.scalar] if e < E - 1 else [nc.sync, nc.scalar] * 2
+            acc = product(w, e, queues, "acc_w")
+            gate = act.tile([P, N], F32, name="gate")
+            nc.scalar.activation(gate[:], acc[:], GELU)
+            if e < E - 1:
+                acc = product(w3, e, [nc.sync, nc.scalar], "acc_w3")
+                nc.vector.tensor_tensor(early_out[:, e, :], acc[:], gate[:], MULT)
 
-                acc = psum.tile([P, N], F32, name="acc%d" % matrix)
-                for s in range(PASSES):
-                    grouped = stage.tile([P, N, PACK], BF16, name="grouped", align_bytes=64)
-                    nc.vector.tensor_copy(
-                        out=grouped[:, :VECTOR_COLUMNS, :].rearrange("p (c i) r -> p c r i", i=RUN),
-                        in_=raw[:, s, :, :VECTOR_COLUMNS].rearrange("p r (c i) -> p c r i", i=RUN),
-                    )
-                    nc.scalar.copy(
-                        out=grouped[:, VECTOR_COLUMNS:, :].rearrange("p (c i) r -> p c r i", i=RUN),
-                        in_=raw[:, s, :, VECTOR_COLUMNS:].rearrange("p r (c i) -> p c r i", i=RUN),
-                    )
-                    codes = quant.tile([P, N], U32, name="codes", align_bytes=64)
-                    scales = quant.tile([P, N], U8, name="scales", align_bytes=64)
-                    nc.vector.quantize_mx(
-                        out=codes[:].bitcast(FP8X4),
-                        scales=scales[:],
-                        in_=grouped[:].rearrange("p n r -> p (n r)"),
-                    )
-                    nc.tensor.matmul_mx(
-                        out=acc[:],
-                        lhsT=slot_words[:, s, 2 * C * e : 2 * C * (e + 1)].bitcast(FP4X4),
-                        lhsT_scale=slot_scales[:, s, C * e : C * (e + 1)],
-                        rhs=codes[:].bitcast(FP8X4),
-                        rhs_scale=scales[:],
-                        start=(s == 0),
-                        stop=(s == PASSES - 1),
-                    )
-                if matrix == 0:
-                    gate = act.tile([P, N], F32, name="gate")
-                    nc.scalar.activation(gate[:], acc[:], GELU)
-                else:
-                    result = early_out[:, e, :] if e < E - 1 else last_out[:]
-                    nc.vector.tensor_tensor(result, acc[:], gate[:], MULT)
-
+        e = E - 1
+        raws = load(w3, e, [nc.sync] * PASSES)
         nc.sync.dma_start(
-            out=out[: (E - 1) * C, :].rearrange("(e p) n -> p e n", p=P),
+            out=out[: e * C, :].rearrange("(e p) n -> p e n", p=P),
             in_=early_out[:],
         )
-        nc.sync.dma_start(out=out[(E - 1) * C :, :], in_=last_out[:])
+        quarters = [slice(QUARTER * j, QUARTER * (j + 1)) for j in range(4)]
+        accs = [last_psum.tile([P, QUARTER], F32, name="last_acc%d" % j) for j in range(4)]
+        for s in range(PASSES - 1):
+            codes, scales = quantize_pass(raws[s])
+            for j in range(4):
+                multiply(accs[j][:], e, s, codes, scales, quarters[j])
+        s = PASSES - 1
+        grouped, codes, scales = pass_tiles()
+        for j in range(2):
+            interleave(nc.vector.tensor_copy, grouped, raws[s], quarters[j])
+            interleave(nc.scalar.copy, grouped, raws[s], quarters[2 + j])
+        for j in range(4):
+            quantize(grouped, quarters[j], codes, scales)
+            multiply(accs[j][:], e, s, codes, scales, quarters[j])
+        for j in range(4):
+            nc.vector.tensor_tensor(last_out[:, quarters[j]], accs[j][:], gate[:, quarters[j]], MULT)
+            if j % 2 == 1:
+                columns = slice(QUARTER * (j - 1), QUARTER * (j + 1))
+                nc.sync.dma_start(out=out[e * C :, columns], in_=last_out[:, columns])

@@ -41,7 +41,7 @@ def tile_moe_s_glu_gelu_kernel(tc, x_words, x_scales, w, w3, offs, out):
 
     with ExitStack() as ctx:
         keep = ctx.enter_context(tc.tile_pool(name="keep", bufs=1))
-        raw_pool = ctx.enter_context(tc.tile_pool(name="raw", bufs=8))
+        raw_pool = ctx.enter_context(tc.tile_pool(name="raw", bufs=4))
         stage = ctx.enter_context(tc.tile_pool(name="stage", bufs=4))
         quant = ctx.enter_context(tc.tile_pool(name="quant", bufs=6))
         act = ctx.enter_context(tc.tile_pool(name="act", bufs=2))
@@ -64,10 +64,11 @@ def tile_moe_s_glu_gelu_kernel(tc, x_words, x_scales, w, w3, offs, out):
         nc.sync.dma_start(offsets[:], offs)
 
         nc.vector.memset(token_scales[:].rearrange("p s t -> p (s t)").bitcast(I32), 0)
-        for q in range(4):
+        scale_rows = x_scales.rearrange("s (q r) t -> r q s t", r=4)
+        for r in range(4):
             nc.scalar.dma_start(
-                out=token_scales[32 * q : 32 * q + 4, :, :].bitcast(I32),
-                in_=x_scales[:, 4 * q : 4 * q + 4, :].rearrange("s b t -> b s t").bitcast(I32),
+                out=token_scales[r:P:32, :, :].bitcast(I32),
+                in_=scale_rows[r].bitcast(I32),
             )
 
         for j0 in range(0, SLOTS, GATHER):
@@ -88,17 +89,16 @@ def tile_moe_s_glu_gelu_kernel(tc, x_words, x_scales, w, w3, offs, out):
                 slot_pairs[:, m, :].bitcast(U16).rearrange("p (j q) -> p q j", q=2),
             )
 
-        def load(weights, e, queues):
-            count = PASSES // len(queues)
-            halves = [raw_pool.tile([P, 2, PACK, N], F32, name="raw") for half in range(2)]
-            for d, queue in enumerate(queues):
-                s0 = count * d
+        def load(weights, e, pieces):
+            count = PASSES // pieces
+            raw = raw_pool.tile([P, PASSES, PACK, N], F32, name="raw")
+            for s0 in range(0, PASSES, count):
                 rows = weights[e, K_PASS * s0 : K_PASS * (s0 + count), :]
-                queue.dma_start(
-                    out=halves[s0 // 2][:, s0 % 2 : s0 % 2 + count].rearrange("p s r n -> p s (r n)"),
+                nc.sync.dma_start(
+                    out=raw[:, s0 : s0 + count].rearrange("p s r n -> p s (r n)"),
                     in_=rows.rearrange("(s p r) n -> p s (r n)", p=P, r=PACK),
                 )
-            return [halves[s // 2][:, s % 2] for s in range(PASSES)]
+            return [raw[:, s] for s in range(PASSES)]
 
         def quantize(grouped, columns, codes, scales):
             nc.vector.quantize_mx(
@@ -131,8 +131,8 @@ def tile_moe_s_glu_gelu_kernel(tc, x_words, x_scales, w, w3, offs, out):
             quantize(grouped, slice(0, N), codes, scales)
             return codes, scales
 
-        def product(weights, e, queues, name):
-            raws = load(weights, e, queues)
+        def product(weights, e, pieces, name):
+            raws = load(weights, e, pieces)
             acc = psum.tile([P, N], F32, name=name)
             for s in range(PASSES):
                 codes, scales = quantize_pass(raws[s])
@@ -140,16 +140,16 @@ def tile_moe_s_glu_gelu_kernel(tc, x_words, x_scales, w, w3, offs, out):
             return acc
 
         for e in range(E):
-            queues = [nc.sync, nc.scalar] if e < E - 1 else [nc.sync, nc.scalar] * 2
-            acc = product(w, e, queues, "acc_w")
+            pieces = 1 if e < E - 1 else 2
+            acc = product(w, e, pieces, "acc_w")
             gate = act.tile([P, N], F32, name="gate")
             nc.scalar.activation(gate[:], acc[:], GELU)
             if e < E - 1:
-                acc = product(w3, e, [nc.sync, nc.scalar], "acc_w3")
+                acc = product(w3, e, 1, "acc_w3")
                 nc.vector.tensor_tensor(early_out[:, e, :], acc[:], gate[:], MULT)
 
         e = E - 1
-        raws = load(w3, e, [nc.sync] * PASSES)
+        raws = load(w3, e, PASSES)
         nc.sync.dma_start(
             out=out[: e * C, :].rearrange("(e p) n -> p e n", p=P),
             in_=early_out[:],

@@ -25,6 +25,8 @@ GATHER = 384
 VECTOR_COLUMNS = 256
 RUN = 4
 QUARTER = N // 4
+BURST = 256
+PAGE = 4096
 
 FLOPS = 2 * 2 * SLOTS * K * N
 
@@ -49,13 +51,13 @@ def tile_moe_s_glu_gelu_kernel(tc, x_words, x_scales, w, w3, offs, out):
         last_psum = ctx.enter_context(tc.psum_pool(name="last_psum", bufs=1))
 
         offsets = keep.tile([P, SLOTS // 16], U16, name="offsets")
-        token_words = keep.tile([P, PAIRS, T], I32, name="token_words", align_bytes=64)
-        token_scales = keep.tile([P, PASSES, T], U8, name="token_scales", align_bytes=64)
+        token_words = keep.tile([P, PAIRS, T], I32, name="token_words", align_bytes=BURST)
+        token_scales = keep.tile([P, PASSES, T], U8, name="token_scales", align_bytes=BURST)
         slot_pairs = keep.tile([P, PAIRS, SLOTS], U32, name="slot_pairs", align_bytes=64)
         slot_words = keep.tile([P, PASSES, 2 * SLOTS], U8, name="slot_words", align_bytes=64)
         slot_scales = keep.tile([P, PASSES, SLOTS], U8, name="slot_scales", align_bytes=64)
-        early_out = keep.tile([P, E - 1, N], F32, name="early_out")
-        last_out = keep.tile([P, N], F32, name="last_out")
+        early_out = keep.tile([P, E - 1, N], F32, name="early_out", align_bytes=BURST)
+        last_out = keep.tile([P, N], F32, name="last_out", align_bytes=BURST)
 
         nc.sync.dma_start(
             out=token_words[:],
@@ -91,7 +93,7 @@ def tile_moe_s_glu_gelu_kernel(tc, x_words, x_scales, w, w3, offs, out):
 
         def load(weights, e, pieces):
             count = PASSES // pieces
-            raw = raw_pool.tile([P, PASSES, PACK, N], F32, name="raw")
+            raw = raw_pool.tile([P, PASSES, PACK, N], F32, name="raw", align_bytes=PAGE)
             for s0 in range(0, PASSES, count):
                 rows = weights[e, K_PASS * s0 : K_PASS * (s0 + count), :]
                 nc.sync.dma_start(

@@ -52,7 +52,8 @@ def tile_moe_s_glu_gelu_kernel(tc, x_words, x_scales, w, w3, offs, out):
 
         offsets = keep.tile([P, SLOTS // 16], U16, name="offsets")
         token_words = keep.tile([P, PAIRS, T], I32, name="token_words", align_bytes=BURST)
-        token_scales = keep.tile([P, PASSES, T], U8, name="token_scales", align_bytes=BURST)
+        landed_scales = keep.tile([P, PASSES * T], U8, name="landed_scales", align_bytes=BURST)
+        token_scales = keep.tile([P, PASSES, T], U8, name="token_scales", align_bytes=64)
         slot_pairs = keep.tile([P, PAIRS, SLOTS], U32, name="slot_pairs", align_bytes=64)
         slot_words = keep.tile([P, PASSES, 2 * SLOTS], U8, name="slot_words", align_bytes=64)
         slot_scales = keep.tile([P, PASSES, SLOTS], U8, name="slot_scales", align_bytes=64)
@@ -65,13 +66,18 @@ def tile_moe_s_glu_gelu_kernel(tc, x_words, x_scales, w, w3, offs, out):
         )
         nc.sync.dma_start(offsets[:], offs)
 
-        nc.vector.memset(token_scales[:].rearrange("p s t -> p (s t)").bitcast(I32), 0)
         scale_rows = x_scales.rearrange("s (q r) t -> r q s t", r=4)
+        landed = landed_scales[:].rearrange("p (s t) -> p s t", s=PASSES)
         for r in range(4):
-            nc.scalar.dma_start(
-                out=token_scales[r:P:32, :, :].bitcast(I32),
+            nc.sync.dma_start(
+                out=landed[r:P:32, :, :].bitcast(I32),
                 in_=scale_rows[r].bitcast(I32),
             )
+        planes = token_scales[:].rearrange("p s t -> p (s t)").bitcast(I32)
+        nc.vector.memset(planes, 0)
+        for q in range(4):
+            live = slice(32 * q, 32 * q + 4)
+            nc.vector.tensor_copy(planes[live, :], landed_scales[live, :].bitcast(I32))
 
         for j0 in range(0, SLOTS, GATHER):
             piece = offsets[:, j0 // 16 : (j0 + GATHER) // 16]
@@ -142,31 +148,40 @@ def tile_moe_s_glu_gelu_kernel(tc, x_words, x_scales, w, w3, offs, out):
             return acc
 
         for e in range(E):
-            pieces = 1 if e < E - 1 else 2
+            pieces = 1 if e < E - 1 else PASSES
             acc = product(w, e, pieces, "acc_w")
             gate = act.tile([P, N], F32, name="gate")
             nc.scalar.activation(gate[:], acc[:], GELU)
             if e < E - 1:
-                acc = product(w3, e, 1, "acc_w3")
+                acc = product(w3, e, 1 if e < E - 2 else 2, "acc_w3")
                 nc.vector.tensor_tensor(early_out[:, e, :], acc[:], gate[:], MULT)
 
         e = E - 1
-        raws = load(w3, e, PASSES)
+        s = PASSES - 1
+        raw = raw_pool.tile([P, PASSES, PACK, N], F32, name="raw", align_bytes=PAGE)
+        rows = w3[e].rearrange("(s p r) n -> s p r n", p=P, r=PACK)
+        for s0 in range(s):
+            nc.sync.dma_start(out=raw[:, s0], in_=rows[s0])
+        pairs = [slice(0, 2), slice(2, 4)]
+        for pair in pairs:
+            nc.sync.dma_start(out=raw[:, s, pair, :], in_=rows[s][:, pair, :])
         nc.sync.dma_start(
             out=out[: e * C, :].rearrange("(e p) n -> p e n", p=P),
             in_=early_out[:],
         )
         quarters = [slice(QUARTER * j, QUARTER * (j + 1)) for j in range(4)]
         accs = [last_psum.tile([P, QUARTER], F32, name="last_acc%d" % j) for j in range(4)]
-        for s in range(PASSES - 1):
-            codes, scales = quantize_pass(raws[s])
+        for s0 in range(s):
+            codes, scales = quantize_pass(raw[:, s0])
             for j in range(4):
-                multiply(accs[j][:], e, s, codes, scales, quarters[j])
-        s = PASSES - 1
+                multiply(accs[j][:], e, s0, codes, scales, quarters[j])
         grouped, codes, scales = pass_tiles()
+        first, second = pairs
+        interleave(nc.vector.tensor_copy, grouped[:, :, first], raw[:, s, first, :], slice(0, VECTOR_COLUMNS))
+        interleave(nc.scalar.copy, grouped[:, :, first], raw[:, s, first, :], slice(VECTOR_COLUMNS, N))
         for j in range(2):
-            interleave(nc.vector.tensor_copy, grouped, raws[s], quarters[j])
-            interleave(nc.scalar.copy, grouped, raws[s], quarters[2 + j])
+            interleave(nc.vector.tensor_copy, grouped[:, :, second], raw[:, s, second, :], quarters[j])
+            interleave(nc.scalar.copy, grouped[:, :, second], raw[:, s, second, :], quarters[2 + j])
         for j in range(4):
             quantize(grouped, quarters[j], codes, scales)
             multiply(accs[j][:], e, s, codes, scales, quarters[j])

@@ -27,6 +27,10 @@ RUN = 4
 QUARTER = N // 4
 BURST = 256
 PAGE = 4096
+MATRIX_PASSES = E * PASSES
+LOADS_W = [9, 8, 7]
+LOADS_W3 = [6, 5, 4, 3, 2, 1, 1, 1]
+RING = 18
 
 FLOPS = 2 * 2 * SLOTS * K * N
 
@@ -43,10 +47,8 @@ def tile_moe_s_glu_gelu_kernel(tc, x_words, x_scales, w, w3, offs, out):
 
     with ExitStack() as ctx:
         keep = ctx.enter_context(tc.tile_pool(name="keep", bufs=1))
-        raw_pool = ctx.enter_context(tc.tile_pool(name="raw", bufs=4))
         stage = ctx.enter_context(tc.tile_pool(name="stage", bufs=4))
         quant = ctx.enter_context(tc.tile_pool(name="quant", bufs=6))
-        act = ctx.enter_context(tc.tile_pool(name="act", bufs=2))
         psum = ctx.enter_context(tc.psum_pool(name="psum", bufs=2))
         last_psum = ctx.enter_context(tc.psum_pool(name="last_psum", bufs=1))
 
@@ -59,6 +61,8 @@ def tile_moe_s_glu_gelu_kernel(tc, x_words, x_scales, w, w3, offs, out):
         slot_scales = keep.tile([P, PASSES, SLOTS], U8, name="slot_scales", align_bytes=64)
         early_out = keep.tile([P, E - 1, N], F32, name="early_out", align_bytes=BURST)
         last_out = keep.tile([P, N], F32, name="last_out", align_bytes=BURST)
+        gates = keep.tile([P, E, N], F32, name="gates")
+        ring = keep.tile([P, RING, PACK, N], F32, name="ring", align_bytes=PAGE)
 
         nc.sync.dma_start(
             out=token_words[:],
@@ -97,16 +101,13 @@ def tile_moe_s_glu_gelu_kernel(tc, x_words, x_scales, w, w3, offs, out):
                 slot_pairs[:, m, :].bitcast(U16).rearrange("p (j q) -> p q j", q=2),
             )
 
-        def load(weights, e, pieces):
-            count = PASSES // pieces
-            raw = raw_pool.tile([P, PASSES, PACK, N], F32, name="raw", align_bytes=PAGE)
-            for s0 in range(0, PASSES, count):
-                rows = weights[e, K_PASS * s0 : K_PASS * (s0 + count), :]
-                nc.sync.dma_start(
-                    out=raw[:, s0 : s0 + count].rearrange("p s r n -> p s (r n)"),
-                    in_=rows.rearrange("(s p r) n -> p s (r n)", p=P, r=PACK),
-                )
-            return [raw[:, s] for s in range(PASSES)]
+        def load(rows, first_pass, count, place):
+            nc.sync.dma_start(
+                out=ring[:, place : place + count].rearrange("p s r n -> p s (r n)"),
+                in_=rows[K_PASS * first_pass : K_PASS * (first_pass + count), :].rearrange(
+                    "(s p r) n -> p s (r n)", p=P, r=PACK
+                ),
+            )
 
         def quantize(grouped, columns, codes, scales):
             nc.vector.quantize_mx(
@@ -139,54 +140,61 @@ def tile_moe_s_glu_gelu_kernel(tc, x_words, x_scales, w, w3, offs, out):
             quantize(grouped, slice(0, N), codes, scales)
             return codes, scales
 
-        def product(weights, e, pieces, name):
-            raws = load(weights, e, pieces)
-            acc = psum.tile([P, N], F32, name=name)
-            for s in range(PASSES):
-                codes, scales = quantize_pass(raws[s])
-                multiply(acc[:], e, s, codes, scales, slice(0, N))
-            return acc
+        quarters = [slice(QUARTER * j, QUARTER * (j + 1)) for j in range(4)]
+        last_accs = [last_psum.tile([P, QUARTER], F32, name="last_acc%d" % j) for j in range(4)]
 
-        for e in range(E):
-            pieces = 1 if e < E - 1 else PASSES
-            acc = product(w, e, pieces, "acc_w")
-            gate = act.tile([P, N], F32, name="gate")
-            nc.scalar.activation(gate[:], acc[:], GELU)
-            if e < E - 1:
-                acc = product(w3, e, 1 if e < E - 2 else 2, "acc_w3")
-                nc.vector.tensor_tensor(early_out[:, e, :], acc[:], gate[:], MULT)
+        def finish_gate(acc, e):
+            nc.scalar.activation(gates[:, e, :], acc[:], GELU)
+
+        def finish_product(acc, e):
+            nc.vector.tensor_tensor(early_out[:, e, :], acc[:], gates[:, e, :], MULT)
+
+        place = 0
+        for weights, counts, finish in ((w, LOADS_W, finish_gate), (w3, LOADS_W3, finish_product)):
+            rows = weights.rearrange("e k n -> (e k) n")
+            done = 0
+            for count in counts:
+                if place + count > RING:
+                    place = 0
+                load(rows, done, count, place)
+                for i in range(count):
+                    e, s = divmod(done + i, PASSES)
+                    codes, scales = quantize_pass(ring[:, place + i])
+                    if finish is finish_product and e == E - 1:
+                        for j in range(4):
+                            multiply(last_accs[j][:], e, s, codes, scales, quarters[j])
+                    else:
+                        if s == 0:
+                            acc = psum.tile([P, N], F32, name="acc")
+                        multiply(acc[:], e, s, codes, scales, slice(0, N))
+                        if s == PASSES - 1:
+                            finish(acc, e)
+                done = done + count
+                place = place + count
 
         e = E - 1
         s = PASSES - 1
-        raw = raw_pool.tile([P, PASSES, PACK, N], F32, name="raw", align_bytes=PAGE)
-        rows = w3[e].rearrange("(s p r) n -> s p r n", p=P, r=PACK)
-        for s0 in range(s):
-            nc.sync.dma_start(out=raw[:, s0], in_=rows[s0])
+        raw = ring[:, place]
+        last_rows = w3[e, K_PASS * s :, :].rearrange("(p r) n -> p r n", r=PACK)
         pairs = [slice(0, 2), slice(2, 4)]
         for pair in pairs:
-            nc.sync.dma_start(out=raw[:, s, pair, :], in_=rows[s][:, pair, :])
+            nc.sync.dma_start(out=raw[:, pair, :], in_=last_rows[:, pair, :])
         nc.sync.dma_start(
             out=out[: e * C, :].rearrange("(e p) n -> p e n", p=P),
             in_=early_out[:],
         )
-        quarters = [slice(QUARTER * j, QUARTER * (j + 1)) for j in range(4)]
-        accs = [last_psum.tile([P, QUARTER], F32, name="last_acc%d" % j) for j in range(4)]
-        for s0 in range(s):
-            codes, scales = quantize_pass(raw[:, s0])
-            for j in range(4):
-                multiply(accs[j][:], e, s0, codes, scales, quarters[j])
         grouped, codes, scales = pass_tiles()
         first, second = pairs
-        interleave(nc.vector.tensor_copy, grouped[:, :, first], raw[:, s, first, :], slice(0, VECTOR_COLUMNS))
-        interleave(nc.scalar.copy, grouped[:, :, first], raw[:, s, first, :], slice(VECTOR_COLUMNS, N))
+        interleave(nc.vector.tensor_copy, grouped[:, :, first], raw[:, first, :], slice(0, VECTOR_COLUMNS))
+        interleave(nc.scalar.copy, grouped[:, :, first], raw[:, first, :], slice(VECTOR_COLUMNS, N))
         for j in range(2):
-            interleave(nc.vector.tensor_copy, grouped[:, :, second], raw[:, s, second, :], quarters[j])
-            interleave(nc.scalar.copy, grouped[:, :, second], raw[:, s, second, :], quarters[2 + j])
+            interleave(nc.vector.tensor_copy, grouped[:, :, second], raw[:, second, :], quarters[j])
+            interleave(nc.scalar.copy, grouped[:, :, second], raw[:, second, :], quarters[2 + j])
         for j in range(4):
             quantize(grouped, quarters[j], codes, scales)
-            multiply(accs[j][:], e, s, codes, scales, quarters[j])
+            multiply(last_accs[j][:], e, s, codes, scales, quarters[j])
         for j in range(4):
-            nc.vector.tensor_tensor(last_out[:, quarters[j]], accs[j][:], gate[:, quarters[j]], MULT)
+            nc.vector.tensor_tensor(last_out[:, quarters[j]], last_accs[j][:], gates[:, e, quarters[j]], MULT)
             if j % 2 == 1:
                 columns = slice(QUARTER * (j - 1), QUARTER * (j + 1))
                 nc.sync.dma_start(out=out[e * C :, columns], in_=last_out[:, columns])

@@ -64,12 +64,6 @@ def tile_moe_s_glu_gelu_kernel(tc, x_words, x_scales, w, w3, offs, out):
         gates = keep.tile([P, E, N], F32, name="gates")
         ring = keep.tile([P, RING, PACK, N], F32, name="ring", align_bytes=PAGE)
 
-        nc.sync.dma_start(
-            out=token_words[:],
-            in_=x_words.rearrange("m p t d -> p m (t d)").bitcast(I32),
-        )
-        nc.sync.dma_start(offsets[:], offs)
-
         scale_rows = x_scales.rearrange("s (q r) t -> r q s t", r=4)
         landed = landed_scales[:].rearrange("p (s t) -> p s t", s=PASSES)
         for r in range(4):
@@ -77,6 +71,12 @@ def tile_moe_s_glu_gelu_kernel(tc, x_words, x_scales, w, w3, offs, out):
                 out=landed[r:P:32, :, :].bitcast(I32),
                 in_=scale_rows[r].bitcast(I32),
             )
+        nc.sync.dma_start(
+            out=token_words[:],
+            in_=x_words.rearrange("m p t d -> p m (t d)").bitcast(I32),
+        )
+        nc.sync.dma_start(offsets[:], offs)
+
         planes = token_scales[:].rearrange("p s t -> p (s t)").bitcast(I32)
         nc.vector.memset(planes, 0)
         for q in range(4):
@@ -195,6 +195,6 @@ def tile_moe_s_glu_gelu_kernel(tc, x_words, x_scales, w, w3, offs, out):
             multiply(last_accs[j][:], e, s, codes, scales, quarters[j])
         for j in range(4):
             nc.vector.tensor_tensor(last_out[:, quarters[j]], last_accs[j][:], gates[:, e, quarters[j]], MULT)
-            if j % 2 == 1:
-                columns = slice(QUARTER * (j - 1), QUARTER * (j + 1))
+            if j > 0:
+                columns = slice(0 if j == 1 else QUARTER * j, QUARTER * (j + 1))
                 nc.sync.dma_start(out=out[e * C :, columns], in_=last_out[:, columns])

@@ -25,6 +25,7 @@ GATHER = 384
 VECTOR_COLUMNS = 256
 RUN = 4
 QUARTER = N // 4
+HALF = N // 2
 BURST = 256
 PAGE = 4096
 MATRIX_PASSES = E * PASSES
@@ -60,9 +61,14 @@ def tile_moe_s_glu_gelu_kernel(tc, x_words, x_scales, w, w3, offs, out):
         slot_words = keep.tile([P, PASSES, 2 * SLOTS], U8, name="slot_words", align_bytes=64)
         slot_scales = keep.tile([P, PASSES, SLOTS], U8, name="slot_scales", align_bytes=64)
         early_out = keep.tile([P, E - 1, N], F32, name="early_out", align_bytes=BURST)
-        last_out = keep.tile([P, N], F32, name="last_out", align_bytes=BURST)
         gates = keep.tile([P, E, N], F32, name="gates")
-        ring = keep.tile([P, RING, PACK, N], F32, name="ring", align_bytes=PAGE)
+        ring = keep.tile([P, RING * PACK * N], F32, name="ring", align_bytes=PAGE)
+
+        nc.sync.dma_start(
+            out=token_words[:],
+            in_=x_words.rearrange("m p t d -> p m (t d)").bitcast(I32),
+        )
+        nc.sync.dma_start(offsets[:], offs)
 
         scale_rows = x_scales.rearrange("s (q r) t -> r q s t", r=4)
         landed = landed_scales[:].rearrange("p (s t) -> p s t", s=PASSES)
@@ -71,12 +77,6 @@ def tile_moe_s_glu_gelu_kernel(tc, x_words, x_scales, w, w3, offs, out):
                 out=landed[r:P:32, :, :].bitcast(I32),
                 in_=scale_rows[r].bitcast(I32),
             )
-        nc.sync.dma_start(
-            out=token_words[:],
-            in_=x_words.rearrange("m p t d -> p m (t d)").bitcast(I32),
-        )
-        nc.sync.dma_start(offsets[:], offs)
-
         planes = token_scales[:].rearrange("p s t -> p (s t)").bitcast(I32)
         nc.vector.memset(planes, 0)
         for q in range(4):
@@ -101,9 +101,16 @@ def tile_moe_s_glu_gelu_kernel(tc, x_words, x_scales, w, w3, offs, out):
                 slot_pairs[:, m, :].bitcast(U16).rearrange("p (j q) -> p q j", q=2),
             )
 
+        def landing(place):
+            return ring[:, PACK * N * place : PACK * N * (place + 1)].rearrange("p (r n) -> p r n", r=PACK)
+
+        def staged_in(place):
+            start = PACK * N * place
+            return ring[:, start : start + PACK * N // 2].bitcast(BF16).rearrange("p (n r) -> p n r", r=PACK)
+
         def load(rows, first_pass, count, place):
             nc.sync.dma_start(
-                out=ring[:, place : place + count].rearrange("p s r n -> p s (r n)"),
+                out=ring[:, PACK * N * place : PACK * N * (place + count)].rearrange("p (s x) -> p s x", s=count),
                 in_=rows[K_PASS * first_pass : K_PASS * (first_pass + count), :].rearrange(
                     "(s p r) n -> p s (r n)", p=P, r=PACK
                 ),
@@ -127,16 +134,15 @@ def tile_moe_s_glu_gelu_kernel(tc, x_words, x_scales, w, w3, offs, out):
                 stop=(s == PASSES - 1),
             )
 
-        def pass_tiles():
-            grouped = stage.tile([P, N, PACK], BF16, name="grouped", align_bytes=64)
+        def code_tiles():
             codes = quant.tile([P, N], U32, name="codes", align_bytes=64)
             scales = quant.tile([P, N], U8, name="scales", align_bytes=64)
-            return grouped, codes, scales
+            return codes, scales
 
-        def quantize_pass(raw):
-            grouped, codes, scales = pass_tiles()
-            interleave(nc.vector.tensor_copy, grouped, raw, slice(0, VECTOR_COLUMNS))
-            interleave(nc.scalar.copy, grouped, raw, slice(VECTOR_COLUMNS, N))
+        def quantize_pass(raw, grouped, share):
+            codes, scales = code_tiles()
+            interleave(nc.vector.tensor_copy, grouped, raw, slice(0, share))
+            interleave(nc.scalar.copy, grouped, raw, slice(share, N))
             quantize(grouped, slice(0, N), codes, scales)
             return codes, scales
 
@@ -159,7 +165,8 @@ def tile_moe_s_glu_gelu_kernel(tc, x_words, x_scales, w, w3, offs, out):
                 load(rows, done, count, place)
                 for i in range(count):
                     e, s = divmod(done + i, PASSES)
-                    codes, scales = quantize_pass(ring[:, place + i])
+                    grouped = stage.tile([P, N, PACK], BF16, name="grouped", align_bytes=64)
+                    codes, scales = quantize_pass(landing(place + i), grouped[:], VECTOR_COLUMNS)
                     if finish is finish_product and e == E - 1:
                         for j in range(4):
                             multiply(last_accs[j][:], e, s, codes, scales, quarters[j])
@@ -174,27 +181,34 @@ def tile_moe_s_glu_gelu_kernel(tc, x_words, x_scales, w, w3, offs, out):
 
         e = E - 1
         s = PASSES - 1
-        raw = ring[:, place]
-        last_rows = w3[e, K_PASS * s :, :].rearrange("(p r) n -> p r n", r=PACK)
-        pairs = [slice(0, 2), slice(2, 4)]
-        for pair in pairs:
-            nc.sync.dma_start(out=raw[:, pair, :], in_=last_rows[:, pair, :])
+        start = PACK * N * place
+        raws = []
+        for h in range(2):
+            raw = ring[:, start + PACK * HALF * h : start + PACK * HALF * (h + 1)].rearrange("p (r n) -> p r n", r=PACK)
+            rows = w3[e, K_PASS * s :, HALF * h : HALF * (h + 1)]
+            nc.sync.dma_start(out=raw, in_=rows.rearrange("(p r) n -> p r n", r=PACK))
+            raws.append(raw)
         nc.sync.dma_start(
             out=out[: e * C, :].rearrange("(e p) n -> p e n", p=P),
             in_=early_out[:],
         )
-        grouped, codes, scales = pass_tiles()
-        first, second = pairs
-        interleave(nc.vector.tensor_copy, grouped[:, :, first], raw[:, first, :], slice(0, VECTOR_COLUMNS))
-        interleave(nc.scalar.copy, grouped[:, :, first], raw[:, first, :], slice(VECTOR_COLUMNS, N))
+        left = stage.tile([P, HALF, PACK], BF16, name="grouped", align_bytes=64)
+        right = ring[:, start : start + PACK * HALF // 2].bitcast(BF16).rearrange("p (n r) -> p n r", r=PACK)
+        codes, scales = code_tiles()
+        interleave(nc.vector.tensor_copy, left[:], raws[0], quarters[0])
+        interleave(nc.scalar.copy, left[:], raws[0], quarters[1])
+        quantize(left[:], slice(0, HALF), codes, scales)
         for j in range(2):
-            interleave(nc.vector.tensor_copy, grouped[:, :, second], raw[:, second, :], quarters[j])
-            interleave(nc.scalar.copy, grouped[:, :, second], raw[:, second, :], quarters[2 + j])
-        for j in range(4):
-            quantize(grouped, quarters[j], codes, scales)
             multiply(last_accs[j][:], e, s, codes, scales, quarters[j])
+        codes, scales = code_tiles()
+        interleave(nc.vector.tensor_copy, right, raws[1], quarters[0])
+        interleave(nc.scalar.copy, right, raws[1], quarters[1])
+        for j in range(2):
+            quantize(right, quarters[j], codes, scales)
+            multiply(last_accs[2 + j][:], e, s, codes, scales, quarters[j])
+        last_out = ring[:, start : start + N]
         for j in range(4):
             nc.vector.tensor_tensor(last_out[:, quarters[j]], last_accs[j][:], gates[:, e, quarters[j]], MULT)
-            if j > 0:
-                columns = slice(0 if j == 1 else QUARTER * j, QUARTER * (j + 1))
+            if j % 2 == 1:
+                columns = slice(QUARTER * (j - 1), QUARTER * (j + 1))
                 nc.sync.dma_start(out=out[e * C :, columns], in_=last_out[:, columns])

@@ -26,6 +26,7 @@ VECTOR_COLUMNS = 256
 RUN = 4
 QUARTER = N // 4
 HALF = N // 2
+LAST_COLUMNS = 96
 BURST = 256
 PAGE = 4096
 MATRIX_PASSES = E * PASSES
@@ -183,10 +184,9 @@ def tile_moe_s_glu_gelu_kernel(tc, x_words, x_scales, w, w3, offs, out):
         s = PASSES - 1
         start = PACK * N * place
         raws = []
-        for h in range(2):
-            raw = ring[:, start + PACK * HALF * h : start + PACK * HALF * (h + 1)].rearrange("p (r n) -> p r n", r=PACK)
-            rows = w3[e, K_PASS * s :, HALF * h : HALF * (h + 1)]
-            nc.sync.dma_start(out=raw, in_=rows.rearrange("(p r) n -> p r n", r=PACK))
+        for columns in (slice(0, HALF), quarters[2], quarters[3]):
+            raw = ring[:, start + PACK * columns.start : start + PACK * columns.stop].rearrange("p (r n) -> p r n", r=PACK)
+            nc.sync.dma_start(out=raw, in_=w3[e, K_PASS * s :, columns].rearrange("(p r) n -> p r n", r=PACK))
             raws.append(raw)
         nc.sync.dma_start(
             out=out[: e * C, :].rearrange("(e p) n -> p e n", p=P),
@@ -201,14 +201,15 @@ def tile_moe_s_glu_gelu_kernel(tc, x_words, x_scales, w, w3, offs, out):
         for j in range(2):
             multiply(last_accs[j][:], e, s, codes, scales, quarters[j])
         codes, scales = code_tiles()
-        interleave(nc.vector.tensor_copy, right, raws[1], quarters[0])
-        interleave(nc.scalar.copy, right, raws[1], quarters[1])
+        interleave(nc.scalar.copy, right[:, quarters[0], :], raws[1], quarters[0])
+        interleave(nc.vector.tensor_copy, right[:, quarters[1], :], raws[2], slice(0, LAST_COLUMNS))
+        interleave(nc.scalar.copy, right[:, quarters[1], :], raws[2], slice(LAST_COLUMNS, QUARTER))
         for j in range(2):
             quantize(right, quarters[j], codes, scales)
             multiply(last_accs[2 + j][:], e, s, codes, scales, quarters[j])
         last_out = ring[:, start : start + N]
         for j in range(4):
             nc.vector.tensor_tensor(last_out[:, quarters[j]], last_accs[j][:], gates[:, e, quarters[j]], MULT)
-            if j % 2 == 1:
-                columns = slice(QUARTER * (j - 1), QUARTER * (j + 1))
+            if j > 0:
+                columns = slice(0 if j == 1 else QUARTER * j, QUARTER * (j + 1))
                 nc.sync.dma_start(out=out[e * C :, columns], in_=last_out[:, columns])

@@ -23,16 +23,17 @@ PASSES = K // K_PASS
 PAIRS = PASSES // 2
 GATHER = 384
 VECTOR_COLUMNS = 256
+VECTOR_COLUMNS_IN_RUN = 232
 RUN = 4
 QUARTER = N // 4
 HALF = N // 2
 LAST_COLUMNS = 96
 BURST = 256
-PAGE = 4096
+RING_ALIGN = 4096
 MATRIX_PASSES = E * PASSES
-LOADS_W = [9, 8, 7]
-LOADS_W3 = [6, 5, 4, 3, 2, 1, 1, 1]
-RING = 18
+LOADS = [(0, 10), (0, 10), (1, 9), (1, 6), (1, 5), (0, 2), (0, 2), (1, 1), (1, 1), (1, 1)]
+RING = 20
+PLACE = PACK * N
 
 FLOPS = 2 * 2 * SLOTS * K * N
 
@@ -50,20 +51,20 @@ def tile_moe_s_glu_gelu_kernel(tc, x_words, x_scales, w, w3, offs, out):
     with ExitStack() as ctx:
         keep = ctx.enter_context(tc.tile_pool(name="keep", bufs=1))
         stage = ctx.enter_context(tc.tile_pool(name="stage", bufs=4))
-        quant = ctx.enter_context(tc.tile_pool(name="quant", bufs=6))
+        quant = ctx.enter_context(tc.tile_pool(name="quant", bufs=4))
+        shared = ctx.enter_context(tc.tile_pool(name="shared", bufs=1))
         psum = ctx.enter_context(tc.psum_pool(name="psum", bufs=2))
         last_psum = ctx.enter_context(tc.psum_pool(name="last_psum", bufs=1))
 
         offsets = keep.tile([P, SLOTS // 16], U16, name="offsets")
-        token_words = keep.tile([P, PAIRS, T], I32, name="token_words", align_bytes=BURST)
-        landed_scales = keep.tile([P, PASSES * T], U8, name="landed_scales", align_bytes=BURST)
         token_scales = keep.tile([P, PASSES, T], U8, name="token_scales", align_bytes=64)
-        slot_pairs = keep.tile([P, PAIRS, SLOTS], U32, name="slot_pairs", align_bytes=64)
         slot_words = keep.tile([P, PASSES, 2 * SLOTS], U8, name="slot_words", align_bytes=64)
         slot_scales = keep.tile([P, PASSES, SLOTS], U8, name="slot_scales", align_bytes=64)
-        early_out = keep.tile([P, E - 1, N], F32, name="early_out", align_bytes=BURST)
-        gates = keep.tile([P, E, N], F32, name="gates")
-        ring = keep.tile([P, RING * PACK * N], F32, name="ring", align_bytes=PAGE)
+        ring = keep.tile([P, RING * PLACE], F32, name="ring", align_bytes=RING_ALIGN)
+        token_words = shared.tile([P, PAIRS, T], I32, name="token_words", align_bytes=BURST, offset=0)
+        landed_scales = shared.tile([P, PASSES * T], U8, name="landed_scales", align_bytes=BURST, offset=4 * PAIRS * T)
+        slot_pairs = shared.tile([P, PAIRS, SLOTS], U32, name="slot_pairs", align_bytes=BURST, offset=(4 * PAIRS + PASSES) * T)
+        gates = shared.tile([P, E, N], F32, name="gates", align_bytes=BURST, offset=0)
 
         nc.sync.dma_start(
             out=token_words[:],
@@ -102,27 +103,33 @@ def tile_moe_s_glu_gelu_kernel(tc, x_words, x_scales, w, w3, offs, out):
                 slot_pairs[:, m, :].bitcast(U16).rearrange("p (j q) -> p q j", q=2),
             )
 
-        def landing(place):
-            return ring[:, PACK * N * place : PACK * N * (place + 1)].rearrange("p (r n) -> p r n", r=PACK)
+        def landed_at(word, width):
+            return ring[:, word : word + PACK * width].rearrange("p (r n) -> p r n", r=PACK)
 
-        def staged_in(place):
-            start = PACK * N * place
-            return ring[:, start : start + PACK * N // 2].bitcast(BF16).rearrange("p (n r) -> p n r", r=PACK)
+        def staged_at(word, width):
+            return ring[:, word : word + PACK * width // 2].bitcast(BF16).rearrange("p (n r) -> p n r", r=PACK)
 
         def load(rows, first_pass, count, place):
             nc.sync.dma_start(
-                out=ring[:, PACK * N * place : PACK * N * (place + count)].rearrange("p (s x) -> p s x", s=count),
+                out=ring[:, PLACE * place : PLACE * (place + count)].rearrange("p (s x) -> p s x", s=count),
                 in_=rows[K_PASS * first_pass : K_PASS * (first_pass + count), :].rearrange(
                     "(s p r) n -> p s (r n)", p=P, r=PACK
                 ),
             )
 
-        def quantize(grouped, columns, codes, scales):
+        def cast(raw, grouped, on_vector, on_scalar):
+            interleave(nc.vector.tensor_copy, grouped, raw, on_vector)
+            interleave(nc.scalar.copy, grouped, raw, on_scalar)
+
+        def quantize(grouped, width):
+            codes = quant.tile([P, N], U32, name="codes", align_bytes=64)
+            scales = quant.tile([P, N], U8, name="scales", align_bytes=64)
             nc.vector.quantize_mx(
-                out=codes[:, columns].bitcast(FP8X4),
-                scales=scales[:, columns],
-                in_=grouped[:, columns, :].rearrange("p n r -> p (n r)"),
+                out=codes[:, :width].bitcast(FP8X4),
+                scales=scales[:, :width],
+                in_=grouped.rearrange("p n r -> p (n r)"),
             )
+            return codes, scales
 
         def multiply(acc, e, s, codes, scales, columns):
             nc.tensor.matmul_mx(
@@ -135,81 +142,70 @@ def tile_moe_s_glu_gelu_kernel(tc, x_words, x_scales, w, w3, offs, out):
                 stop=(s == PASSES - 1),
             )
 
-        def code_tiles():
-            codes = quant.tile([P, N], U32, name="codes", align_bytes=64)
-            scales = quant.tile([P, N], U8, name="scales", align_bytes=64)
-            return codes, scales
-
-        def quantize_pass(raw, grouped, share):
-            codes, scales = code_tiles()
-            interleave(nc.vector.tensor_copy, grouped, raw, slice(0, share))
-            interleave(nc.scalar.copy, grouped, raw, slice(share, N))
-            quantize(grouped, slice(0, N), codes, scales)
-            return codes, scales
-
         quarters = [slice(QUARTER * j, QUARTER * (j + 1)) for j in range(4)]
         last_accs = [last_psum.tile([P, QUARTER], F32, name="last_acc%d" % j) for j in range(4)]
+
+        def multiply_quarters(first, count, s, codes, scales):
+            for j in range(count):
+                multiply(last_accs[first + j][:], E - 1, s, codes, scales, quarters[j])
 
         def finish_gate(acc, e):
             nc.scalar.activation(gates[:, e, :], acc[:], GELU)
 
         def finish_product(acc, e):
-            nc.vector.tensor_tensor(early_out[:, e, :], acc[:], gates[:, e, :], MULT)
+            nc.vector.tensor_tensor(gates[:, e, :], acc[:], gates[:, e, :], MULT)
 
         place = 0
-        for weights, counts, finish in ((w, LOADS_W, finish_gate), (w3, LOADS_W3, finish_product)):
-            rows = weights.rearrange("e k n -> (e k) n")
-            done = 0
-            for count in counts:
-                if place + count > RING:
-                    place = 0
-                load(rows, done, count, place)
-                for i in range(count):
-                    e, s = divmod(done + i, PASSES)
-                    grouped = stage.tile([P, N, PACK], BF16, name="grouped", align_bytes=64)
-                    codes, scales = quantize_pass(landing(place + i), grouped[:], VECTOR_COLUMNS)
-                    if finish is finish_product and e == E - 1:
-                        for j in range(4):
-                            multiply(last_accs[j][:], e, s, codes, scales, quarters[j])
-                    else:
-                        if s == 0:
-                            acc = psum.tile([P, N], F32, name="acc")
-                        multiply(acc[:], e, s, codes, scales, slice(0, N))
-                        if s == PASSES - 1:
-                            finish(acc, e)
-                done = done + count
-                place = place + count
+        done = [0, 0]
+        for branch, count in LOADS:
+            if place + count > RING:
+                place = 0
+            load((w, w3)[branch].rearrange("e k n -> (e k) n"), done[branch], count, place)
+            share = VECTOR_COLUMNS if count == 1 else VECTOR_COLUMNS_IN_RUN
+            for i in range(count):
+                e, s = divmod(done[branch] + i, PASSES)
+                staged = stage.tile([P, N, PACK], BF16, name="staged", align_bytes=64)
+                cast(landed_at(PLACE * (place + i), N), staged[:], slice(0, share), slice(share, N))
+                codes, scales = quantize(staged[:], N)
+                if branch == 1 and e == E - 1:
+                    multiply_quarters(0, 4, s, codes, scales)
+                else:
+                    if s == 0:
+                        acc = psum.tile([P, N], F32, name="acc")
+                    multiply(acc[:], e, s, codes, scales, slice(0, N))
+                    if s == PASSES - 1:
+                        (finish_gate, finish_product)[branch](acc, e)
+            done[branch] = done[branch] + count
+            place = place + count
 
         e = E - 1
         s = PASSES - 1
-        start = PACK * N * place
+        start = PLACE * place
         raws = []
         for columns in (slice(0, HALF), quarters[2], quarters[3]):
-            raw = ring[:, start + PACK * columns.start : start + PACK * columns.stop].rearrange("p (r n) -> p r n", r=PACK)
+            raw = landed_at(start + PACK * columns.start, columns.stop - columns.start)
             nc.sync.dma_start(out=raw, in_=w3[e, K_PASS * s :, columns].rearrange("(p r) n -> p r n", r=PACK))
             raws.append(raw)
         nc.sync.dma_start(
             out=out[: e * C, :].rearrange("(e p) n -> p e n", p=P),
-            in_=early_out[:],
+            in_=gates[:, :e, :],
         )
-        left = stage.tile([P, HALF, PACK], BF16, name="grouped", align_bytes=64)
-        right = ring[:, start : start + PACK * HALF // 2].bitcast(BF16).rearrange("p (n r) -> p n r", r=PACK)
-        codes, scales = code_tiles()
-        interleave(nc.vector.tensor_copy, left[:], raws[0], quarters[0])
-        interleave(nc.scalar.copy, left[:], raws[0], quarters[1])
-        quantize(left[:], slice(0, HALF), codes, scales)
-        for j in range(2):
-            multiply(last_accs[j][:], e, s, codes, scales, quarters[j])
-        codes, scales = code_tiles()
-        interleave(nc.scalar.copy, right[:, quarters[0], :], raws[1], quarters[0])
-        interleave(nc.vector.tensor_copy, right[:, quarters[1], :], raws[2], slice(0, LAST_COLUMNS))
-        interleave(nc.scalar.copy, right[:, quarters[1], :], raws[2], slice(LAST_COLUMNS, QUARTER))
-        for j in range(2):
-            quantize(right, quarters[j], codes, scales)
-            multiply(last_accs[2 + j][:], e, s, codes, scales, quarters[j])
-        last_out = ring[:, start : start + N]
+        left = stage.tile([P, HALF, PACK], BF16, name="staged", align_bytes=64)
+        cast(raws[0], left[:], quarters[0], quarters[1])
+        codes, scales = quantize(left[:], HALF)
+        multiply_quarters(0, 2, s, codes, scales)
+        stagings = [start, start + HALF]
+        third, fourth = [staged_at(word, QUARTER) for word in stagings]
+        interleave(nc.scalar.copy, third, raws[1], quarters[0])
+        cast(raws[2], fourth, slice(0, LAST_COLUMNS), slice(LAST_COLUMNS, QUARTER))
+        for j, grouped in ((2, third), (3, fourth)):
+            codes, scales = quantize(grouped, QUARTER)
+            multiply_quarters(j, 1, s, codes, scales)
+        results = [ring[:, staging : staging + HALF] for staging in stagings]
         for j in range(4):
-            nc.vector.tensor_tensor(last_out[:, quarters[j]], last_accs[j][:], gates[:, e, quarters[j]], MULT)
-            if j > 0:
-                columns = slice(0 if j == 1 else QUARTER * j, QUARTER * (j + 1))
-                nc.sync.dma_start(out=out[e * C :, columns], in_=last_out[:, columns])
+            result = results[j // 2][:, quarters[j % 2]]
+            nc.vector.tensor_tensor(result, last_accs[j][:], gates[:, e, quarters[j]], MULT)
+            if j == 1:
+                nc.sync.dma_start(out=out[e * C :, :HALF], in_=results[0])
+            if j > 1:
+                nc.sync.dma_start(out=out[e * C :, quarters[j]], in_=result)

@@ -23,8 +23,9 @@ PASSES = K // K_PASS
 PAIRS = PASSES // 2
 GATHER = 384
 VECTOR_COLUMNS = 256
-VECTOR_COLUMNS_IN_RUN = 232
+VECTOR_COLUMNS_IN_RUN = 240
 RUN = 4
+GATE_BEHIND = 1
 QUARTER = N // 4
 HALF = N // 2
 LAST_COLUMNS = 96
@@ -64,7 +65,7 @@ def tile_moe_s_glu_gelu_kernel(tc, x_words, x_scales, w, w3, offs, out):
         token_words = shared.tile([P, PAIRS, T], I32, name="token_words", align_bytes=BURST, offset=0)
         landed_scales = shared.tile([P, PASSES * T], U8, name="landed_scales", align_bytes=BURST, offset=4 * PAIRS * T)
         slot_pairs = shared.tile([P, PAIRS, SLOTS], U32, name="slot_pairs", align_bytes=BURST, offset=(4 * PAIRS + PASSES) * T)
-        gates = shared.tile([P, E, N], F32, name="gates", align_bytes=BURST, offset=0)
+        gates = shared.tile([P, E - 1, N], F32, name="gates", align_bytes=BURST, offset=0)
 
         nc.sync.dma_start(
             out=token_words[:],
@@ -169,11 +170,14 @@ def tile_moe_s_glu_gelu_kernel(tc, x_words, x_scales, w, w3, offs, out):
                 codes, scales = quantize(staged[:], N)
                 if branch == 1 and e == E - 1:
                     multiply_quarters(0, 4, s, codes, scales)
+                    if s == GATE_BEHIND:
+                        last_gate = ring[:, PLACE * (place + 1) - N : PLACE * (place + 1)]
+                        nc.scalar.activation(last_gate, acc[:], GELU)
                 else:
                     if s == 0:
                         acc = psum.tile([P, N], F32, name="acc")
                     multiply(acc[:], e, s, codes, scales, slice(0, N))
-                    if s == PASSES - 1:
+                    if s == PASSES - 1 and e < E - 1:
                         (finish_gate, finish_product)[branch](acc, e)
             done[branch] = done[branch] + count
             place = place + count
@@ -188,7 +192,7 @@ def tile_moe_s_glu_gelu_kernel(tc, x_words, x_scales, w, w3, offs, out):
             raws.append(raw)
         nc.sync.dma_start(
             out=out[: e * C, :].rearrange("(e p) n -> p e n", p=P),
-            in_=gates[:, :e, :],
+            in_=gates[:],
         )
         left = stage.tile([P, HALF, PACK], BF16, name="staged", align_bytes=64)
         cast(raws[0], left[:], quarters[0], quarters[1])
@@ -204,7 +208,7 @@ def tile_moe_s_glu_gelu_kernel(tc, x_words, x_scales, w, w3, offs, out):
         results = [ring[:, staging : staging + HALF] for staging in stagings]
         for j in range(4):
             result = results[j // 2][:, quarters[j % 2]]
-            nc.vector.tensor_tensor(result, last_accs[j][:], gates[:, e, quarters[j]], MULT)
+            nc.vector.tensor_tensor(result, last_accs[j][:], last_gate[:, quarters[j]], MULT)
             if j == 1:
                 nc.sync.dma_start(out=out[e * C :, :HALF], in_=results[0])
             if j > 1:

@@ -53,7 +53,6 @@ def tile_moe_s_glu_gelu_kernel(tc, x_words, x_scales, w, w3, offs, out):
         keep = ctx.enter_context(tc.tile_pool(name="keep", bufs=1))
         stage = ctx.enter_context(tc.tile_pool(name="stage", bufs=4))
         quant = ctx.enter_context(tc.tile_pool(name="quant", bufs=4))
-        shared = ctx.enter_context(tc.tile_pool(name="shared", bufs=1))
         psum = ctx.enter_context(tc.psum_pool(name="psum", bufs=2))
         last_psum = ctx.enter_context(tc.psum_pool(name="last_psum", bufs=1))
 
@@ -61,11 +60,11 @@ def tile_moe_s_glu_gelu_kernel(tc, x_words, x_scales, w, w3, offs, out):
         token_scales = keep.tile([P, PASSES, T], U8, name="token_scales", align_bytes=64)
         slot_words = keep.tile([P, PASSES, 2 * SLOTS], U8, name="slot_words", align_bytes=64)
         slot_scales = keep.tile([P, PASSES, SLOTS], U8, name="slot_scales", align_bytes=64)
+        token_words = keep.tile([P, PAIRS, T], I32, name="token_words", align_bytes=BURST)
+        landed_scales = keep.tile([P, PASSES * T], U8, name="landed_scales", align_bytes=BURST)
+        slot_pairs = keep.tile([P, PAIRS, SLOTS], U32, name="slot_pairs", align_bytes=BURST)
+        gates = keep.tile([P, E - 1, N], F32, name="gates", align_bytes=BURST)
         ring = keep.tile([P, RING * PLACE], F32, name="ring", align_bytes=RING_ALIGN)
-        token_words = shared.tile([P, PAIRS, T], I32, name="token_words", align_bytes=BURST, offset=0)
-        landed_scales = shared.tile([P, PASSES * T], U8, name="landed_scales", align_bytes=BURST, offset=4 * PAIRS * T)
-        slot_pairs = shared.tile([P, PAIRS, SLOTS], U32, name="slot_pairs", align_bytes=BURST, offset=(4 * PAIRS + PASSES) * T)
-        gates = shared.tile([P, E - 1, N], F32, name="gates", align_bytes=BURST, offset=0)
 
         nc.sync.dma_start(
             out=token_words[:],

@@ -52,7 +52,7 @@ def tile_moe_s_glu_gelu_kernel(tc, x_words, x_scales, w, w3, offs, out):
     with ExitStack() as ctx:
         keep = ctx.enter_context(tc.tile_pool(name="keep", bufs=1))
         stage = ctx.enter_context(tc.tile_pool(name="stage", bufs=4))
-        quant = ctx.enter_context(tc.tile_pool(name="quant", bufs=4))
+        quant = ctx.enter_context(tc.tile_pool(name="quant", bufs=6))
         psum = ctx.enter_context(tc.psum_pool(name="psum", bufs=2))
         last_psum = ctx.enter_context(tc.psum_pool(name="last_psum", bufs=1))
 

@@ -166,6 +166,8 @@ def tile_moe_s_glu_gelu_kernel(tc, x_words, x_scales, w, w3, offs, out):
                 e, s = divmod(done[branch] + i, PASSES)
                 staged = stage.tile([P, N, PACK], BF16, name="staged", align_bytes=64)
                 cast(landed_at(PLACE * (place + i), N), staged[:], slice(0, share), slice(share, N))
+                if branch == 1 and done[branch] + i == MATRIX_PASSES - 2:
+                    break
                 codes, scales = quantize(staged[:], N)
                 if branch == 1 and e == E - 1:
                     multiply_quarters(0, 4, s, codes, scales)
@@ -193,8 +195,12 @@ def tile_moe_s_glu_gelu_kernel(tc, x_words, x_scales, w, w3, offs, out):
             out=out[: e * C, :].rearrange("(e p) n -> p e n", p=P),
             in_=gates[:],
         )
+        codes, scales = quantize(staged[:, :HALF, :], HALF)
+        multiply_quarters(0, 2, s - 1, codes, scales)
         left = stage.tile([P, HALF, PACK], BF16, name="staged", align_bytes=64)
         cast(raws[0], left[:], quarters[0], quarters[1])
+        codes, scales = quantize(staged[:, HALF:, :], HALF)
+        multiply_quarters(2, 2, s - 1, codes, scales)
         codes, scales = quantize(left[:], HALF)
         multiply_quarters(0, 2, s, codes, scales)
         stagings = [start, start + HALF]

@@ -32,7 +32,7 @@ LAST_COLUMNS = 96
 BURST = 256
 RING_ALIGN = 4096
 MATRIX_PASSES = E * PASSES
-LOADS = [(0, 10), (0, 10), (1, 9), (1, 6), (1, 5), (0, 2), (0, 2), (1, 1), (1, 1), (1, 1)]
+LOADS = [(0, 10), (0, 10), (1, 7), (1, 6), (1, 4), (1, 3), (0, 2), (0, 2), (1, 1), (1, 1), (1, 1)]
 RING = 20
 PLACE = PACK * N
 

@@ -143,11 +143,16 @@ def tile_moe_s_glu_gelu_kernel(tc, x_words, x_scales, w, w3, offs, out):
             )
 
         quarters = [slice(QUARTER * j, QUARTER * (j + 1)) for j in range(4)]
-        last_accs = [last_psum.tile([P, QUARTER], F32, name="last_acc%d" % j) for j in range(4)]
+        pieces = [slice(0, HALF), quarters[2], quarters[3]]
+        last_accs = [
+            last_psum.tile([P, piece.stop - piece.start], F32, name="last_acc%d" % j) for j, piece in enumerate(pieces)
+        ]
 
-        def multiply_quarters(first, count, s, codes, scales):
-            for j in range(count):
-                multiply(last_accs[first + j][:], E - 1, s, codes, scales, quarters[j])
+        def multiply_pieces(chosen, s, codes, scales):
+            first = pieces[chosen[0]].start
+            for j in chosen:
+                columns = slice(pieces[j].start - first, pieces[j].stop - first)
+                multiply(last_accs[j][:], E - 1, s, codes, scales, columns)
 
         def finish_gate(acc, e):
             nc.scalar.activation(gates[:, e, :], acc[:], GELU)
@@ -170,7 +175,7 @@ def tile_moe_s_glu_gelu_kernel(tc, x_words, x_scales, w, w3, offs, out):
                     break
                 codes, scales = quantize(staged[:], N)
                 if branch == 1 and e == E - 1:
-                    multiply_quarters(0, 4, s, codes, scales)
+                    multiply_pieces((0, 1, 2), s, codes, scales)
                     if s == GATE_BEHIND:
                         last_gate = ring[:, PLACE * (place + 1) - N : PLACE * (place + 1)]
                         nc.scalar.activation(last_gate, acc[:], GELU)
@@ -187,7 +192,7 @@ def tile_moe_s_glu_gelu_kernel(tc, x_words, x_scales, w, w3, offs, out):
         s = PASSES - 1
         start = PLACE * place
         raws = []
-        for columns in (slice(0, HALF), quarters[2], quarters[3]):
+        for columns in pieces:
             raw = landed_at(start + PACK * columns.start, columns.stop - columns.start)
             nc.sync.dma_start(out=raw, in_=w3[e, K_PASS * s :, columns].rearrange("(p r) n -> p r n", r=PACK))
             raws.append(raw)
@@ -196,25 +201,21 @@ def tile_moe_s_glu_gelu_kernel(tc, x_words, x_scales, w, w3, offs, out):
             in_=gates[:],
         )
         codes, scales = quantize(staged[:, :HALF, :], HALF)
-        multiply_quarters(0, 2, s - 1, codes, scales)
+        multiply_pieces((0,), s - 1, codes, scales)
         left = stage.tile([P, HALF, PACK], BF16, name="staged", align_bytes=64)
         cast(raws[0], left[:], quarters[0], quarters[1])
         codes, scales = quantize(staged[:, HALF:, :], HALF)
-        multiply_quarters(2, 2, s - 1, codes, scales)
+        multiply_pieces((1, 2), s - 1, codes, scales)
         codes, scales = quantize(left[:], HALF)
-        multiply_quarters(0, 2, s, codes, scales)
+        multiply_pieces((0,), s, codes, scales)
         stagings = [start, start + HALF]
         third, fourth = [staged_at(word, QUARTER) for word in stagings]
         interleave(nc.scalar.copy, third, raws[1], quarters[0])
         cast(raws[2], fourth, slice(0, LAST_COLUMNS), slice(LAST_COLUMNS, QUARTER))
-        for j, grouped in ((2, third), (3, fourth)):
+        for j, grouped in ((1, third), (2, fourth)):
             codes, scales = quantize(grouped, QUARTER)
-            multiply_quarters(j, 1, s, codes, scales)
-        results = [ring[:, staging : staging + HALF] for staging in stagings]
-        for j in range(4):
-            result = results[j // 2][:, quarters[j % 2]]
-            nc.vector.tensor_tensor(result, last_accs[j][:], last_gate[:, quarters[j]], MULT)
-            if j == 1:
-                nc.sync.dma_start(out=out[e * C :, :HALF], in_=results[0])
-            if j > 1:
-                nc.sync.dma_start(out=out[e * C :, quarters[j]], in_=result)
+            multiply_pieces((j,), s, codes, scales)
+        results = ring[:, start : start + N]
+        for j, piece in enumerate(pieces):
+            nc.vector.tensor_tensor(results[:, piece], last_accs[j][:], last_gate[:, piece], MULT)
+            nc.sync.dma_start(out=out[e * C :, piece], in_=results[:, piece])

@@ -32,8 +32,8 @@ LAST_COLUMNS = 96
 BURST = 256
 RING_ALIGN = 4096
 MATRIX_PASSES = E * PASSES
-LOADS = [(0, 10), (0, 10), (1, 7), (1, 6), (1, 4), (1, 3), (0, 2), (0, 2), (1, 1), (1, 1), (1, 1)]
-RING = 20
+LOADS = [(0, 12), (1, 10), (0, 8), (1, 6), (1, 4), (0, 2), (0, 2), (1, 1), (1, 1), (1, 1)]
+RING = 22
 PLACE = PACK * N
 
 FLOPS = 2 * 2 * SLOTS * K * N
@@ -51,6 +51,7 @@ def tile_moe_s_glu_gelu_kernel(tc, x_words, x_scales, w, w3, offs, out):
 
     with ExitStack() as ctx:
         keep = ctx.enter_context(tc.tile_pool(name="keep", bufs=1))
+        shared = ctx.enter_context(tc.tile_pool(name="shared", bufs=1))
         stage = ctx.enter_context(tc.tile_pool(name="stage", bufs=4))
         quant = ctx.enter_context(tc.tile_pool(name="quant", bufs=6))
         psum = ctx.enter_context(tc.psum_pool(name="psum", bufs=2))
@@ -60,10 +61,10 @@ def tile_moe_s_glu_gelu_kernel(tc, x_words, x_scales, w, w3, offs, out):
         token_scales = keep.tile([P, PASSES, T], U8, name="token_scales", align_bytes=64)
         slot_words = keep.tile([P, PASSES, 2 * SLOTS], U8, name="slot_words", align_bytes=64)
         slot_scales = keep.tile([P, PASSES, SLOTS], U8, name="slot_scales", align_bytes=64)
-        token_words = keep.tile([P, PAIRS, T], I32, name="token_words", align_bytes=BURST)
+        token_words = shared.tile([P, PAIRS, T], I32, name="token_words", align_bytes=BURST, offset=0)
         landed_scales = keep.tile([P, PASSES * T], U8, name="landed_scales", align_bytes=BURST)
-        slot_pairs = keep.tile([P, PAIRS, SLOTS], U32, name="slot_pairs", align_bytes=BURST)
-        gates = keep.tile([P, E - 1, N], F32, name="gates", align_bytes=BURST)
+        slot_pairs = shared.tile([P, PAIRS, SLOTS], U32, name="slot_pairs", align_bytes=BURST, offset=4 * PAIRS * T)
+        gates = shared.tile([P, E - 1, N], F32, name="gates", align_bytes=BURST, offset=0)
         ring = keep.tile([P, RING * PLACE], F32, name="ring", align_bytes=RING_ALIGN)
 
         nc.sync.dma_start(
@@ -162,6 +163,7 @@ def tile_moe_s_glu_gelu_kernel(tc, x_words, x_scales, w, w3, offs, out):
 
         place = 0
         done = [0, 0]
+        accs = [None, None]
         for branch, count in LOADS:
             if place + count > RING:
                 place = 0
@@ -178,13 +180,13 @@ def tile_moe_s_glu_gelu_kernel(tc, x_words, x_scales, w, w3, offs, out):
                     multiply_pieces((0, 1, 2), s, codes, scales)
                     if s == GATE_BEHIND:
                         last_gate = ring[:, PLACE * (place + 1) - N : PLACE * (place + 1)]
-                        nc.scalar.activation(last_gate, acc[:], GELU)
+                        nc.scalar.activation(last_gate, accs[0][:], GELU)
                 else:
                     if s == 0:
-                        acc = psum.tile([P, N], F32, name="acc")
-                    multiply(acc[:], e, s, codes, scales, slice(0, N))
+                        accs[branch] = psum.tile([P, N], F32, name="acc%d" % branch)
+                    multiply(accs[branch][:], e, s, codes, scales, slice(0, N))
                     if s == PASSES - 1 and e < E - 1:
-                        (finish_gate, finish_product)[branch](acc, e)
+                        (finish_gate, finish_product)[branch](accs[branch], e)
             done[branch] = done[branch] + count
             place = place + count
 

@@ -33,6 +33,7 @@ BURST = 256
 RING_ALIGN = 4096
 MATRIX_PASSES = E * PASSES
 LOADS = [(0, 12), (1, 10), (0, 8), (1, 6), (1, 4), (0, 2), (0, 2), (1, 1), (1, 1), (1, 1)]
+FIRST_STORE = 3
 RING = 22
 PLACE = PACK * N
 
@@ -198,10 +199,11 @@ def tile_moe_s_glu_gelu_kernel(tc, x_words, x_scales, w, w3, offs, out):
             raw = landed_at(start + PACK * columns.start, columns.stop - columns.start)
             nc.sync.dma_start(out=raw, in_=w3[e, K_PASS * s :, columns].rearrange("(p r) n -> p r n", r=PACK))
             raws.append(raw)
-        nc.sync.dma_start(
-            out=out[: e * C, :].rearrange("(e p) n -> p e n", p=P),
-            in_=gates[:],
-        )
+        for experts in (slice(0, FIRST_STORE), slice(FIRST_STORE, e)):
+            nc.sync.dma_start(
+                out=out[experts.start * C : experts.stop * C, :].rearrange("(e p) n -> p e n", p=P),
+                in_=gates[:, experts, :],
+            )
         codes, scales = quantize(staged[:, :HALF, :], HALF)
         multiply_pieces((0,), s - 1, codes, scales)
         left = stage.tile([P, HALF, PACK], BF16, name="staged", align_bytes=64)

@@ -23,12 +23,14 @@ PASSES = K // K_PASS
 PAIRS = PASSES // 2
 GATHER = 384
 VECTOR_COLUMNS = 256
+VECTOR_COLUMNS_LAST_WHOLE = 288
+VECTOR_COLUMNS_LEFT = 144
 VECTOR_COLUMNS_IN_RUN = 240
 RUN = 4
 GATE_BEHIND = 1
 QUARTER = N // 4
 HALF = N // 2
-LAST_COLUMNS = 96
+LAST_COLUMNS = 32
 BURST = 256
 RING_ALIGN = 4096
 MATRIX_PASSES = E * PASSES
@@ -173,9 +175,12 @@ def tile_moe_s_glu_gelu_kernel(tc, x_words, x_scales, w, w3, offs, out):
             for i in range(count):
                 e, s = divmod(done[branch] + i, PASSES)
                 staged = stage.tile([P, N, PACK], BF16, name="staged", align_bytes=64)
-                cast(landed_at(PLACE * (place + i), N), staged[:], slice(0, share), slice(share, N))
+                raw = landed_at(PLACE * (place + i), N)
                 if branch == 1 and done[branch] + i == MATRIX_PASSES - 2:
+                    cast(raw, staged[:], slice(0, VECTOR_COLUMNS_LAST_WHOLE), quarters[3])
+                    interleave(nc.scalar.copy, staged[:], raw, slice(VECTOR_COLUMNS_LAST_WHOLE, quarters[3].start))
                     break
+                cast(raw, staged[:], slice(0, share), slice(share, N))
                 codes, scales = quantize(staged[:], N)
                 if branch == 1 and e == E - 1:
                     multiply_pieces((0, 1, 2), s, codes, scales)
@@ -204,22 +209,25 @@ def tile_moe_s_glu_gelu_kernel(tc, x_words, x_scales, w, w3, offs, out):
                 out=out[experts.start * C : experts.stop * C, :].rearrange("(e p) n -> p e n", p=P),
                 in_=gates[:, experts, :],
             )
-        codes, scales = quantize(staged[:, :HALF, :], HALF)
+        codes, scales = quantize(staged[:, pieces[2], :], QUARTER)
+        multiply_pieces((2,), s - 1, codes, scales)
+        codes, scales = quantize(staged[:, pieces[0], :], HALF)
         multiply_pieces((0,), s - 1, codes, scales)
         left = stage.tile([P, HALF, PACK], BF16, name="staged", align_bytes=64)
-        cast(raws[0], left[:], quarters[0], quarters[1])
-        codes, scales = quantize(staged[:, HALF:, :], HALF)
-        multiply_pieces((1, 2), s - 1, codes, scales)
+        cast(raws[0], left[:], slice(0, VECTOR_COLUMNS_LEFT), slice(VECTOR_COLUMNS_LEFT, HALF))
+        codes, scales = quantize(staged[:, pieces[1], :], QUARTER)
+        multiply_pieces((1,), s - 1, codes, scales)
         codes, scales = quantize(left[:], HALF)
         multiply_pieces((0,), s, codes, scales)
-        stagings = [start, start + HALF]
+        stagings = [start + PLACE, start + PLACE + HALF]
         third, fourth = [staged_at(word, QUARTER) for word in stagings]
         interleave(nc.scalar.copy, third, raws[1], quarters[0])
         cast(raws[2], fourth, slice(0, LAST_COLUMNS), slice(LAST_COLUMNS, QUARTER))
         for j, grouped in ((1, third), (2, fourth)):
             codes, scales = quantize(grouped, QUARTER)
             multiply_pieces((j,), s, codes, scales)
-        results = ring[:, start : start + N]
+        words = [start + PLACE - N, start + PLACE - HALF, start]
         for j, piece in enumerate(pieces):
-            nc.vector.tensor_tensor(results[:, piece], last_accs[j][:], last_gate[:, piece], MULT)
-            nc.sync.dma_start(out=out[e * C :, piece], in_=results[:, piece])
+            result = ring[:, words[j] : words[j] + piece.stop - piece.start]
+            nc.vector.tensor_tensor(result, last_accs[j][:], last_gate[:, piece], MULT)
+            nc.sync.dma_start(out=out[e * C :, piece], in_=result)

@@ -23,14 +23,14 @@ PASSES = K // K_PASS
 PAIRS = PASSES // 2
 GATHER = 384
 VECTOR_COLUMNS = 256
-VECTOR_COLUMNS_LAST_WHOLE = 288
-VECTOR_COLUMNS_LEFT = 144
+VECTOR_COLUMNS_LAST_WHOLE = 256
+VECTOR_COLUMNS_LEFT = 160
 VECTOR_COLUMNS_IN_RUN = 240
 RUN = 4
 GATE_BEHIND = 1
 QUARTER = N // 4
 HALF = N // 2
-LAST_COLUMNS = 32
+LAST_COLUMNS = 48
 BURST = 256
 RING_ALIGN = 4096
 MATRIX_PASSES = E * PASSES

@@ -181,12 +181,17 @@ def tile_moe_s_glu_gelu_kernel(tc, x_words, x_scales, w, w3, offs, out):
                     interleave(nc.scalar.copy, staged[:], raw, slice(VECTOR_COLUMNS_LAST_WHOLE, quarters[3].start))
                     break
                 cast(raw, staged[:], slice(0, share), slice(share, N))
+                if branch == 1 and e == E - 1 and s == GATE_BEHIND:
+                    codes, scales = quantize(staged[:, :HALF, :], HALF)
+                    multiply_pieces((0,), s, codes, scales)
+                    codes, scales = quantize(staged[:, HALF:, :], HALF)
+                    multiply_pieces((1, 2), s, codes, scales)
+                    last_gate = ring[:, PLACE * (place + 1) - N : PLACE * (place + 1)]
+                    nc.scalar.activation(last_gate, accs[0][:], GELU)
+                    continue
                 codes, scales = quantize(staged[:], N)
                 if branch == 1 and e == E - 1:
                     multiply_pieces((0, 1, 2), s, codes, scales)
-                    if s == GATE_BEHIND:
-                        last_gate = ring[:, PLACE * (place + 1) - N : PLACE * (place + 1)]
-                        nc.scalar.activation(last_gate, accs[0][:], GELU)
                 else:
                     if s == 0:
                         accs[branch] = psum.tile([P, N], F32, name="acc%d" % branch)

from contextlib import ExitStack

import concourse.mybir as mybir

K, T, E, C, N = 2048, 512, 6, 128, 512
SLOTS = E * C

F32 = mybir.dt.float32
BF16 = mybir.dt.bfloat16
I32 = mybir.dt.int32
U32 = mybir.dt.uint32
U16 = mybir.dt.uint16
U8 = mybir.dt.uint8
FP8X4 = mybir.dt.float8_e4m3fn_x4
FP4X4 = mybir.dt.float4_e2m1fn_x4
GELU = mybir.ActivationFunctionType.Gelu_apprx_tanh
MULT = mybir.AluOpType.mult

P = 128
PACK = 4
K_PASS = P * PACK
PASSES = K // K_PASS
PAIRS = PASSES // 2
GATHER = 384
VECTOR_COLUMNS = 256
VECTOR_COLUMNS_LAST_WHOLE = 256
VECTOR_COLUMNS_LEFT = 160
VECTOR_COLUMNS_IN_RUN = 240
RUN = 4
GATE_BEHIND = 1
QUARTER = N // 4
HALF = N // 2
LAST_COLUMNS = 48
BURST = 256
RING_ALIGN = 4096
MATRIX_PASSES = E * PASSES
LOADS = [(0, 12), (1, 10), (0, 8), (1, 6), (1, 4), (0, 2), (0, 2), (1, 1), (1, 1), (1, 1)]
FIRST_STORE = 3
RING = 22
PLACE = PACK * N

FLOPS = 2 * 2 * SLOTS * K * N


def interleave(copy, grouped, raw, columns):
    copy(
        out=grouped[:, columns, :].rearrange("p (c i) r -> p c r i", i=RUN),
        in_=raw[:, :, columns].rearrange("p r (c i) -> p c r i", i=RUN),
    )


def tile_moe_s_glu_gelu_kernel(tc, x_words, x_scales, w, w3, offs, out):
    nc = tc.nc

    with ExitStack() as ctx:
        keep = ctx.enter_context(tc.tile_pool(name="keep", bufs=1))
        shared = ctx.enter_context(tc.tile_pool(name="shared", bufs=1))
        stage = ctx.enter_context(tc.tile_pool(name="stage", bufs=4))
        quant = ctx.enter_context(tc.tile_pool(name="quant", bufs=6))
        psum = ctx.enter_context(tc.psum_pool(name="psum", bufs=2))
        last_psum = ctx.enter_context(tc.psum_pool(name="last_psum", bufs=1))

        offsets = keep.tile([P, SLOTS // 16], U16, name="offsets")
        token_scales = keep.tile([P, PASSES, T], U8, name="token_scales", align_bytes=64)
        slot_words = keep.tile([P, PASSES, 2 * SLOTS], U8, name="slot_words", align_bytes=64)
        slot_scales = keep.tile([P, PASSES, SLOTS], U8, name="slot_scales", align_bytes=64)
        token_words = shared.tile([P, PAIRS, T], I32, name="token_words", align_bytes=BURST, offset=0)
        landed_scales = keep.tile([P, PASSES * T], U8, name="landed_scales", align_bytes=BURST)
        slot_pairs = shared.tile([P, PAIRS, SLOTS], U32, name="slot_pairs", align_bytes=BURST, offset=4 * PAIRS * T)
        gates = shared.tile([P, E - 1, N], F32, name="gates", align_bytes=BURST, offset=0)
        ring = keep.tile([P, RING * PLACE], F32, name="ring", align_bytes=RING_ALIGN)

        nc.sync.dma_start(
            out=token_words[:],
            in_=x_words.rearrange("m p t d -> p m (t d)").bitcast(I32),
        )
        nc.sync.dma_start(offsets[:], offs)

        scale_rows = x_scales.rearrange("s (q r) t -> r q s t", r=4)
        landed = landed_scales[:].rearrange("p (s t) -> p s t", s=PASSES)
        for r in range(4):
            nc.sync.dma_start(
                out=landed[r:P:32, :, :].bitcast(I32),
                in_=scale_rows[r].bitcast(I32),
            )
        planes = token_scales[:].rearrange("p s t -> p (s t)").bitcast(I32)
        nc.vector.memset(planes, 0)
        for q in range(4):
            live = slice(32 * q, 32 * q + 4)
            nc.vector.tensor_copy(planes[live, :], landed_scales[live, :].bitcast(I32))

        for j0 in range(0, SLOTS, GATHER):
            piece = offsets[:, j0 // 16 : (j0 + GATHER) // 16]
            for m in range(PAIRS):
                nc.vector.tensor_copy(
                    slot_pairs[:, m, j0 : j0 + GATHER],
                    token_words[:, m, :].bitcast(U32).indirect(piece),
                )
            for s in range(PASSES):
                nc.vector.tensor_copy(
                    slot_scales[:, s, j0 : j0 + GATHER],
                    token_scales[:, s, :].indirect(piece),
                )
        for m in range(PAIRS):
            nc.vector.tensor_copy(
                slot_words[:, 2 * m : 2 * m + 2, :].bitcast(U16),
                slot_pairs[:, m, :].bitcast(U16).rearrange("p (j q) -> p q j", q=2),
            )

        def landed_at(word, width):
            return ring[:, word : word + PACK * width].rearrange("p (r n) -> p r n", r=PACK)

        def staged_at(word, width):
            return ring[:, word : word + PACK * width // 2].bitcast(BF16).rearrange("p (n r) -> p n r", r=PACK)

        def load(rows, first_pass, count, place):
            nc.sync.dma_start(
                out=ring[:, PLACE * place : PLACE * (place + count)].rearrange("p (s x) -> p s x", s=count),
                in_=rows[K_PASS * first_pass : K_PASS * (first_pass + count), :].rearrange(
                    "(s p r) n -> p s (r n)", p=P, r=PACK
                ),
            )

        def cast(raw, grouped, on_vector, on_scalar):
            interleave(nc.vector.tensor_copy, grouped, raw, on_vector)
            interleave(nc.scalar.copy, grouped, raw, on_scalar)

        def quantize(grouped, width):
            codes = quant.tile([P, N], U32, name="codes", align_bytes=64)
            scales = quant.tile([P, N], U8, name="scales", align_bytes=64)
            nc.vector.quantize_mx(
                out=codes[:, :width].bitcast(FP8X4),
                scales=scales[:, :width],
                in_=grouped.rearrange("p n r -> p (n r)"),
            )
            return codes, scales

        def multiply(acc, e, s, codes, scales, columns):
            nc.tensor.matmul_mx(
                out=acc,
                lhsT=slot_words[:, s, 2 * C * e : 2 * C * (e + 1)].bitcast(FP4X4),
                lhsT_scale=slot_scales[:, s, C * e : C * (e + 1)],
                rhs=codes[:, columns].bitcast(FP8X4),
                rhs_scale=scales[:, columns],
                start=(s == 0),
                stop=(s == PASSES - 1),
            )

        quarters = [slice(QUARTER * j, QUARTER * (j + 1)) for j in range(4)]
        pieces = [slice(0, HALF), quarters[2], quarters[3]]
        last_accs = [
            last_psum.tile([P, piece.stop - piece.start], F32, name="last_acc%d" % j) for j, piece in enumerate(pieces)
        ]

        def multiply_pieces(chosen, s, codes, scales):
            first = pieces[chosen[0]].start
            for j in chosen:
                columns = slice(pieces[j].start - first, pieces[j].stop - first)
                multiply(last_accs[j][:], E - 1, s, codes, scales, columns)

        def finish_gate(acc, e):
            nc.scalar.activation(gates[:, e, :], acc[:], GELU)

        def finish_product(acc, e):
            nc.vector.tensor_tensor(gates[:, e, :], acc[:], gates[:, e, :], MULT)

        place = 0
        done = [0, 0]
        accs = [None, None]
        for branch, count in LOADS:
            if place + count > RING:
                place = 0
            load((w, w3)[branch].rearrange("e k n -> (e k) n"), done[branch], count, place)
            share = VECTOR_COLUMNS if count == 1 else VECTOR_COLUMNS_IN_RUN
            for i in range(count):
                e, s = divmod(done[branch] + i, PASSES)
                staged = stage.tile([P, N, PACK], BF16, name="staged", align_bytes=64)
                raw = landed_at(PLACE * (place + i), N)
                if branch == 1 and done[branch] + i == MATRIX_PASSES - 2:
                    cast(raw, staged[:], slice(0, VECTOR_COLUMNS_LAST_WHOLE), quarters[3])
                    interleave(nc.scalar.copy, staged[:], raw, slice(VECTOR_COLUMNS_LAST_WHOLE, quarters[3].start))
                    break
                cast(raw, staged[:], slice(0, share), slice(share, N))
                if branch == 1 and e == E - 1 and s == GATE_BEHIND:
                    codes, scales = quantize(staged[:, :HALF, :], HALF)
                    multiply_pieces((0,), s, codes, scales)
                    codes, scales = quantize(staged[:, HALF:, :], HALF)
                    multiply_pieces((1, 2), s, codes, scales)
                    last_gate = ring[:, PLACE * (place + 1) - N : PLACE * (place + 1)]
                    nc.scalar.activation(last_gate, accs[0][:], GELU)
                    continue
                codes, scales = quantize(staged[:], N)
                if branch == 1 and e == E - 1:
                    multiply_pieces((0, 1, 2), s, codes, scales)
                else:
                    if s == 0:
                        accs[branch] = psum.tile([P, N], F32, name="acc%d" % branch)
                    multiply(accs[branch][:], e, s, codes, scales, slice(0, N))
                    if s == PASSES - 1 and e < E - 1:
                        (finish_gate, finish_product)[branch](accs[branch], e)
            done[branch] = done[branch] + count
            place = place + count

        e = E - 1
        s = PASSES - 1
        start = PLACE * place
        raws = []
        for columns in pieces:
            raw = landed_at(start + PACK * columns.start, columns.stop - columns.start)
            nc.sync.dma_start(out=raw, in_=w3[e, K_PASS * s :, columns].rearrange("(p r) n -> p r n", r=PACK))
            raws.append(raw)
        for experts in (slice(0, FIRST_STORE), slice(FIRST_STORE, e)):
            nc.sync.dma_start(
                out=out[experts.start * C : experts.stop * C, :].rearrange("(e p) n -> p e n", p=P),
                in_=gates[:, experts, :],
            )
        codes, scales = quantize(staged[:, pieces[2], :], QUARTER)
        multiply_pieces((2,), s - 1, codes, scales)
        codes, scales = quantize(staged[:, pieces[0], :], HALF)
        multiply_pieces((0,), s - 1, codes, scales)
        left = stage.tile([P, HALF, PACK], BF16, name="staged", align_bytes=64)
        cast(raws[0], left[:], slice(0, VECTOR_COLUMNS_LEFT), slice(VECTOR_COLUMNS_LEFT, HALF))
        codes, scales = quantize(staged[:, pieces[1], :], QUARTER)
        multiply_pieces((1,), s - 1, codes, scales)
        codes, scales = quantize(left[:], HALF)
        multiply_pieces((0,), s, codes, scales)
        stagings = [start + PLACE, start + PLACE + HALF]
        third, fourth = [staged_at(word, QUARTER) for word in stagings]
        interleave(nc.scalar.copy, third, raws[1], quarters[0])
        cast(raws[2], fourth, slice(0, LAST_COLUMNS), slice(LAST_COLUMNS, QUARTER))
        for j, grouped in ((1, third), (2, fourth)):
            codes, scales = quantize(grouped, QUARTER)
            multiply_pieces((j,), s, codes, scales)
        words = [start + PLACE - N, start + PLACE - HALF, start]
        for j, piece in enumerate(pieces):
            result = ring[:, words[j] : words[j] + piece.stop - piece.start]
            nc.vector.tensor_tensor(result, last_accs[j][:], last_gate[:, piece], MULT)
            nc.sync.dma_start(out=out[e * C :, piece], in_=result)
